import numpy as np, ml_dtypes
CORES = [2,6,10,14,18,22,26,30]
N = 8
BF = ml_dtypes.bfloat16
def gentries(a):
    return np.ascontiguousarray(a.reshape(8, 16, -1).transpose(0, 2, 1)).reshape(8, -1)
def gtable(e):
    e = np.asarray(e); return np.ascontiguousarray(e.reshape(8, -1, 16).transpose(0, 2, 1)).reshape(128, -1).astype(np.int32)
T, P, R, CAP = 256, 4096, 3, 128
def put(o):
    return np.stack([gtable(o[r].reshape(8, -1).astype(np.int32)) for r in range(N)])
def get(came):
    return np.stack([gentries(came[r]).reshape(8, R, N - 1, T) for r in range(N)])
def start(rng):
    o = np.stack([rng.permutation(8) for r in range(N)])
    s = np.array([16, 16, 16, 12, 12, 8, 4, 2])[o]; c = np.array([1, 1, 2, 2, 0, 2, 1, 0])[o]
    had = np.array([P // 2, 3 * P // 4, P])[c] + rng.integers(0, np.array([P // 8, P // 4, P + 1])[c])
    n = (rng.integers(0, CAP + 1, (N, 8, R, N - 1)) * s[:, :, None, None]) >> 4
    for r in range(N):
        n[r, rng.integers(0, 8), rng.integers(0, R), rng.integers(0, N - 1)] = 0
        n[r, np.argmax(s[r]), rng.integers(0, R), rng.integers(0, N - 1)] = CAP
    return had[:, :, None].astype(np.int32), n
def consts(rng):
    h = np.zeros((N, 8, 6 * R + 3), np.int32)
    for e in range(R):
        h[:, :, 6 * e:6 * e + 3] = 2 * rng.integers(0, 2048, (N, 8, 3)) + 1
        h[:, :, 6 * e + 3:6 * e + 6] = rng.integers(0, 4096, (N, 8, 3))
    h[:, :, 6 * R:] = 2 * rng.integers(0, 128, (N, 8, 3)) + 1
    return h
def arrivals(rng, n):
    o = np.argsort(np.argsort(rng.random((N, 8, R, N - 1, T)), -1), -1)
    return put(o < n[..., None])
def setup_inputs(rng):
    had, n = start(rng)
    return {"ring": rng.integers(0, 256, (N, 128, P)).astype(np.float32).astype(BF), "had": had, "hc": consts(rng), "came": arrivals(rng, n)}
def setup_inputs_full(rng):
    d = setup_inputs(rng); d["came"] = arrivals(rng, np.full((N, 8, R, N - 1), CAP))
    v = np.array([P // 2, P - 1, P, 2 * P, P + 1, 2 * P - 1, P // 2 + 1, 3 * P // 2])
    d["had"] = np.stack([rng.permutation(v) for r in range(N)])[:, :, None].astype(np.int32); return d
def setup_inputs_lost(rng):
    d = setup_inputs(rng); o = get(d["came"]) > 0; z = rng.integers(0, N)
    for r in range(N):
        w = rng.permutation(8)
        o[r, w[0]] = False
        o[r, w[1]] = False; o[r, w[1], :, :, 0] = True
        o[r, w[2]] = False; o[r, w[2], :, :, T - 1] = True
        o[r, w[3], rng.integers(0, R)] = False
        o[r, w[4], :, :N - 2] = False
    o[z] = False
    d["came"] = put(o); return d
def setup_inputs_ends(rng):
    d = setup_inputs(rng); o = get(d["came"]); hc = d["hc"]
    n0 = np.sum(o[:, :, 0], axis=(2, 3)); v = np.array([P, P - 1, P + 1, 2 * P, 2 * P - 1, P, 2 * P, P + 1])
    d["had"] = (np.stack([rng.permutation(v) for r in range(N)]) - n0)[:, :, None].astype(np.int32)
    a = np.arange(4096); top = int(np.flatnonzero(((2 * ((a * a) & 2047) + a) & 4095) == 4095)[0])
    for q in range(N):
        for e in range(R):
            for g in range(8):
                dd = int(rng.integers(1, N)); r = (q - dd) % N; w = np.flatnonzero(o[r, g, e, dd - 1])
                x = r * T + (int(rng.choice(w)) if w.size else 0)
                for k, u in ((0, 0), (1, top)): hc[q, g, 6 * e + 3 + k] = (u - int(hc[q, g, 6 * e + k]) * x) & 4095
                if g & 1:
                    hc[q, g, 6 * e + 2] = hc[q, g, 6 * e]; hc[q, g, 6 * e + 5] = hc[q, g, 6 * e + 3]
    return d
def setup_inputs_bursts(rng):
    d = setup_inputs(rng); had, n = start(rng); d["had"] = had
    a = rng.integers(0, T - n + 1); b = np.where(rng.random(n.shape) < 0.5, 0, T - n)
    a[:, ::2] = b[:, ::2]; t = np.arange(T)
    d["came"] = put((t >= a[..., None]) & (t < (a + n)[..., None])); return d
def setup_inputs_spread(rng):
    d = setup_inputs(rng)
    d["ring"] = (rng.integers(0, 256, (N, 128, P)) >> rng.integers(0, 9, (N, 1, P))).astype(np.float32).astype(BF)
    d["had"] = rng.integers(P // 2, 2 * P + 1, (N, 8, 1)).astype(np.int32)
    hc = d["hc"]; m = rng.random(hc.shape) < 0.25; lo = np.zeros(6 * R + 3, np.int64); hi = np.full(6 * R + 3, 4095)
    for e in range(R): lo[6 * e:6 * e + 3] = 1
    lo[6 * R:] = 1; hi[6 * R:] = 255
    d["hc"] = np.where(m, np.where(rng.random(hc.shape) < 0.5, lo, hi), hc).astype(np.int32)
    n = np.floor(rng.random((N, 8, R, N - 1)) ** 3 * (CAP + 1)).astype(np.int64)
    d["came"] = arrivals(rng, np.minimum(n, CAP)); return d
def check_inputs(d):
    bad = []; v = d["ring"].astype(np.float32); hc = d["hc"]
    if not ((v >= 0) & (v <= 255) & (v == np.floor(v))).all(): bad.append("ring")
    if not ((d["had"] >= P // 2) & (d["had"] <= 2 * P)).all(): bad.append("had")
    for e in range(R):
        a = hc[:, :, 6 * e:6 * e + 3]; b = hc[:, :, 6 * e + 3:6 * e + 6]
        if not ((a >= 1) & (a <= 4095) & (a & 1 == 1)).all() or not ((b >= 0) & (b <= 4095)).all(): bad.append("hash")
    f = hc[:, :, 6 * R:]
    if not ((f >= 1) & (f <= 255) & (f & 1 == 1)).all(): bad.append("factors")
    if not ((d["came"] == 0) | (d["came"] == 1)).all(): bad.append("flags")
    elif np.max(np.sum(get(d["came"]), axis=-1)) > CAP: bad.append("cap")
    return bad
def reference(ring, had, hc, came):
    y = ring.astype(np.float32).astype(np.int64).reshape(N, 8, 16, P); m = had[:, :, 0].astype(np.int64); h = hc.astype(np.int64)
    fl = get(came) == 1; x = np.arange(N * T)
    for e in range(R):
        pk = np.zeros((N, 8, 16, N * T), np.int64)
        for q in range(N):
            for g in range(8):
                c = min(int(m[q, g]), P)
                for k in range(3):
                    u = (h[q, g, 6 * e + k] * x + h[q, g, 6 * e + 3 + k]) & 4095
                    s = (u * u) & 2047
                    p = (((2 * s + u) & 4095) * c) >> 12
                    pk[q, g] += h[q, g, 6 * R + k] * y[q, g][:, p]
        pk = pk & 255
        for r in range(N):
            for g in range(8):
                for d in range(1, N):
                    keep = pk[(r + d) % N, g][:, r * T:r * T + T][:, fl[r, g, e, d - 1]]; n = keep.shape[1]
                    y[r, g][:, (m[r, g] + np.arange(n)) & (P - 1)] = keep
                    m[r, g] += n
    return {"y": y.reshape(N, 128, P).astype(np.float32), "now": m.reshape(N, 8, 1).astype(np.float32)}

@@ -1,0 +1,573 @@
+import numpy as np
+from concourse.bass import DstId, RemoteDMATransfer
+from concourse.mybir import AluOpType, ActivationFunctionType
+
+N, P, TT, CAP = 8, 4096, 256, 128
+ALU = AluOpType
+ACT = ActivationFunctionType
+F32, BF, I32, U16, F16 = "float32", "bfloat16", "int32", "uint16", "float16"
+CFG = {
+    "sel": ("v", "v", "s"),
+    "nv": ((1, 1, 1, 0, 1, 0, 0), (1, 1, 1, 0, 1, 0, 0), (1, 2, 1, 0, 1, 1, 1)),
+    "calls": ((0,), (1,), (2,), (3,), (4,), (5,), (6,)),
+    "small": ((0, 1, 6), (2, 3), (4, 5)),
+    "cv": "g0 g1 g2 q0 o0 q1 g3 g4 o1 q2 g5 o2 q3 g6 o3 q4 q5 o4 o5 q6 o6", "cs": "g0 g1 g2 g3 g4 g5 g6",
+    "ych": ((0, 256, "s"), (256, 512, "v"), (512, 1024, "s"), (1024, 1536, "v"), (1536, 2048, "s"),
+            (2048, 2560, "v"), (2560, 3072, "s"), (3072, 3584, "v"), (3584, 4096, "s")),
+    "send": 300.0, "lat": 1600.0, "row": 20.0, "first": 2000.0, "tries": 1500, "seed": 1,
+}
+
+
+def sb(shape, d):
+    return ("sbuf", [128] + shape, d)
+
+
+SCRATCH = {
+    "win": sb([P + 3 * 896], BF), "yb": sb([P], F32),
+    "ga0": sb([21 * CAP], BF), "ga1": sb([21 * CAP], BF), "ga2": sb([21 * CAP], BF),
+    "qq": sb([896], I32), "ou0": sb([896], BF), "ou1": sb([896], BF), "ou2": sb([896], BF),
+    "hcr": sb([24], I32), "hcf": sb([24], F32), "hcs": sb([24], F32), "cami": sb([3, 7, 16], I32),
+    "fo": sb([336], BF), "so": sb([336], BF), "fs": sb([7, 2, 16], BF), "fr": sb([7, 2, 16], BF),
+    "fq": sb([224], BF), "sr": sb([224], BF),
+    "msk": sb([112], BF), "pi": sb([4], I32), "col": sb([16], F32),
+    "ti": sb([144], BF), "tg": sb([128], BF), "tabr": sb([2, 56], BF), "tabl": sb([56], BF), "zb": sb([56], BF),
+    "zf": sb([24], F32), "i896": sb([896], BF), "pt": sb([256], F32), "gt": sb([128], F32),
+    "idb": sb([128], BF), "nid": sb([128], BF), "idh": sb([128], F16), "wm": sb([144], BF), "wh": sb([144], BF),
+    "bo": sb([128], BF), "nbo": sb([128], BF), "lt": sb([128], BF), "gm": sb([8], BF),
+    "r1": sb([8], BF), "r16": sb([8], BF), "rh": sb([8], BF), "r8": sb([8], BF), "dg": sb([3, 128], BF),
+    "bq": sb([24], F32), "dl": sb([24], F32), "cd": sb([24], F32), "dj": sb([4], F32), "djr": sb([4], BF),
+    "dja": sb([4], F32), "djb": sb([4], F32), "b2": sb([4], F32), "cc": sb([4], F32), "nw": sb([4], F32),
+    "ct": sb([24], F32), "pw": sb([336], BF), "cm": sb([8, 8, 16], BF), "cn": sb([8, 8, 16], BF),
+    "of1": sb([168], U16), "c2": sb([896], BF), "c3": sb([896], BF), "g2": sb([896], BF),
+    "tl": sb([56], U16), "xl": sb([7, 8], U16),
+    "ha0": sb([7, 3, 8], I32), "hb0": sb([7, 3, 8], I32), "ha1": sb([7, 3, 8], I32), "hb1": sb([7, 3, 8], I32),
+    "ha2": sb([7, 3, 8], I32), "hb2": sb([7, 3, 8], I32),
+    "off0": sb([168], U16), "off1": sb([168], U16), "off2": sb([168], U16), "off3": sb([256], U16),
+    "ja": sb([256], I32), "jb": sb([256], I32), "jh": sb([592], F16), "mk": sb([24, 424], BF),
+}
+for _b in ("pd0", "pd1", "pd2", "pd3", "pa", "pb", "px", "pq"):
+    SCRATCH[_b] = ("psum", [128, 512], F32)
+SEMAPHORES = ["cv", "cs", "cp", "cg", "ldh", "ldc", "ldr", "sty", "ls", "fl", "li", "a0", "a1", "a2"]
+CNT = {"v": "cv", "s": "cs", "p": "cp", "g": "cg"}
+SYNC = 110.0
+
+
+def peers(T, topo, me):
+    a = T.cores[me]
+
+    def key(r):
+        b = T.cores[r]
+        ca, cb = topo.chip(a), topo.chip(b)
+        far = 3 if ca == cb else 2 if topo.mates(ca, cb) else 1 if topo.same_plane(ca, cb) else 0
+        return (far, topo.die(a) == topo.die(b), r)
+    return sorted([r for r in range(N) if r != me], key=key)
+
+
+def engines_for(T, topo, a, b):
+    ca, cb = T.cores[a], T.cores[b]
+    en = topo.engines(ca, cb)
+    if topo.chip(ca) == topo.chip(cb):
+        for c in T.cores:
+            if topo.chip(c) != topo.chip(ca):
+                en = [e for e in en if e not in topo.engines(ca, c)]
+    return en
+
+
+def one_pass(ops, before, after, pr):
+    n = len(ops)
+    left = [len(before[i]) for i in range(n)]
+    rdy, free, fin, t0, order = {}, {}, [0.0] * n, [0.0] * n, []
+
+    def arrive(i):
+        t = 0.0
+        for d in before[i]:
+            same = (ops[d]["q"] == "p" and ops[i]["q"] == "p") or d not in ops[i]["deps"]
+            t = max(t, fin[d] + (-ops[d]["lat"] if same else SYNC if ops[i]["q"] else 0.0))
+        rdy[i] = t
+    for i in range(n):
+        if left[i] == 0:
+            arrive(i)
+    while rdy:
+        e = dict((i, max(rdy[i], free.get(ops[i]["q"], 0.0))) for i in rdy)
+        j = min(rdy, key=lambda i: (e[i], -pr[i], i))
+        q = ops[j]["q"]
+        if q:
+            now = [i for i in rdy if ops[i]["q"] == q and e[i] <= e[j] + 1.0]
+            j = max(now, key=lambda i: (pr[i], -i))
+            soon = [i for i in rdy if ops[i]["q"] == q and pr[i] > pr[j] + 600.0 and e[i] <= e[j] + 0.45 * ops[j]["cost"]]
+            if soon:
+                j = min(soon, key=lambda i: (e[i], i))
+            free[q] = e[j] + ops[j]["cost"]
+        t0[j] = e[j]
+        fin[j] = e[j] + ops[j]["cost"] + ops[j]["lat"]
+        order.append(j)
+        del rdy[j]
+        for k in after[j]:
+            left[k] -= 1
+            if left[k] == 0:
+                arrive(k)
+    return order, t0, fin
+
+
+def rank_of_part(t):
+    if t[:2] in ("ga", "ou", "oq") and t != "out":
+        return (4.0, 7.0, 9.0)[int(t[2])]
+    return {"sel0": 1.0, "cnt": 2.0, "sel1": 5.0, "sel2": 5.5, "hash1_0": 6.0, "tr1": 6.0, "hash2_0": 8.0, "tr2": 8.0,
+            "last": 8.5, "tr3": 8.5, "out": 10.0, "hash0_0": 0.5, "hash0_4": 0.6}.get(t, 0.0)
+
+
+def plan(ops):
+    n = len(ops)
+    deps = [sorted(set(o["deps"] + o["ord"])) for o in ops]
+    kids = [[] for _ in range(n)]
+    for i in range(n):
+        for d in deps[i]:
+            kids[d].append(i)
+    pr = [0.0] * n
+    left, down = [len(k) for k in kids], []
+    todo = [i for i in range(n) if left[i] == 0]
+    while todo:
+        i = todo.pop()
+        down.append(i)
+        for d in deps[i]:
+            left[d] -= 1
+            if left[d] == 0:
+                todo.append(d)
+    for i in down:
+        pr[i] = ops[i]["cost"] + ops[i]["lat"] + max([pr[k] + SYNC for k in kids[i]] + [0.0])
+    rs = np.random.RandomState(CFG["seed"])
+    tags = sorted(set([o["tag"] for o in ops]))
+    tix = [tags.index(o["tag"]) for o in ops]
+    best, off = None, [-1e5 * rank_of_part(t) for t in tags]
+    for it in range(CFG["tries"]):
+        new = list(off)
+        for _ in range(0 if it == 0 else 1 + it % 3):
+            new[int(rs.randint(len(tags)))] += float(rs.normal()) * (1e4, 5e4, 2e5)[it // 3 % 3]
+        up = [new[tix[i]] for i in range(n)]
+        for i in down:
+            for d in deps[i]:
+                up[d] = max(up[d], up[i])
+        order, t0, fin = one_pass(ops, deps, kids, [pr[i] + up[i] for i in range(n)])
+        if best is None or max(fin) <= best[0]:
+            best, off = (max(fin), order, t0), new
+    pr = [-t for t in best[2]]
+    for it in range(CFG["tries"]):
+        new = list(pr)
+        for _ in range(1 + it % 4):
+            k = int(rs.randint(n))
+            dv = float(rs.normal()) * 800.0
+            for i in range(k, min(n, k + 1 + it % 9)):
+                new[i] += dv
+        order, t0, fin = one_pass(ops, deps, kids, new)
+        if max(fin) <= best[0]:
+            best, pr = (max(fin), order, t0), new
+    for i in range(n):
+        ops[i]["t0"] = best[2][i]
+    return best[1]
+
+
+def emit(g, T, ops, order, tail):
+    eng = {"v": g.vector, "s": g.scalar, "p": g.tensor, "g": g, "y": g.sync}
+    pos = dict((j, k) for k, j in enumerate(order))
+    need = set()
+    for j in order:
+        o = ops[j]
+        if o["q"] == "d":
+            o["q"] = None
+        if o["q"] and o["q"] != "p":
+            ds = [d for d in o["deps"] if ops[d]["q"] == "p"]
+            if ds:
+                need.add(max(ds, key=lambda d: pos[d]))
+    cnt = {"v": 0, "s": 0, "p": 0, "g": 0}
+    nxt = None
+    for j in order:
+        o = ops[j]
+        if o["sem"] is None and o["q"]:
+            if o["q"] != "p" or j in need:
+                cnt[o["q"]] += 1
+                o["inc"] = True
+            o["sig"] = (CNT[o["q"]], cnt[o["q"]])
+    for j in reversed(order):
+        o = ops[j]
+        if o["q"] == "p":
+            if o.get("inc"):
+                nxt = o["sig"]
+            else:
+                o["sig"] = nxt
+    known = dict((q, {}) for q in eng)
+    for j in order:
+        o = ops[j]
+        q = o["q"]
+        if not q:
+            o["snap"] = {}
+            continue
+        k = known[q]
+        for d in sorted(o["deps"], key=lambda d: -pos[d]):
+            od = ops[d]
+            if (q == "p" and od["q"] == "p") or od["sem"] == "none":
+                continue
+            s, v = od["sem"] if od["sem"] else od["sig"]
+            if k.get(s, 0) < v:
+                eng[q].wait_ge(T.sem[s], v)
+                k[s] = v
+            for s2, v2 in od["snap"].items():
+                if k.get(s2, 0) < v2:
+                    k[s2] = v2
+        o["snap"] = dict(k)
+        ins = o["fn"](eng[q])
+        if o.get("inc"):
+            ins.then_inc(T.sem[CNT[q]], 1)
+    for q in cnt:
+        g.wait_ge(T.sem[CNT[q]], cnt[q])
+    for s, v in tail:
+        g.wait_ge(T.sem[s], v)
+
+
+def build(T, topo, me):
+    ops, lastw, readers, tag = [], {}, {}, ["tab"]
+
+    def add(q, fn, r=(), w=(), x=(), cost=0.0, lat=0.0, sem=None):
+        deps = set()
+        for k in list(r) + list(x) + list(w):
+            if k in lastw:
+                deps.add(lastw[k])
+        for k in w:
+            deps.update(readers.get(k, []))
+        for k in x:
+            deps.update([i for i in readers.get(k, []) if ops[i]["q"] != q])
+        i = len(ops)
+        ops.append({"q": q, "fn": fn, "deps": sorted(deps), "cost": cost, "lat": lat, "sem": sem, "w": list(w),
+                    "tag": tag[0], "ord": []})
+        for k in list(r) + list(x):
+            readers.setdefault(k, []).append(i)
+        for k in w:
+            lastw[k] = i
+            readers[k] = []
+
+    def vc(n):
+        return 25.0 + 1.04 * max(64.0, n)
+
+    def ts(out, a, s1, s2, o0, o1, n, r, w, x=()):
+        if o1 is None:
+            add("v", lambda e: e.tensor_scalar(out, a, s1, None, o0), r, w, x, vc(n))
+        else:
+            add("v", lambda e: e.tensor_scalar(out, a, s1, s2, o0, o1), r, w, x, vc(n))
+
+    def tt(out, a, b, o, n, r, w, x=()):
+        add("v", lambda e: e.tensor_tensor(out, a, b, o), r, w, x, vc(n))
+
+    def cp(out, a, n, r, w, x=()):
+        add("v", lambda e: e.tensor_copy(out, a), r, w, x, vc(n))
+
+    def ms(out, v, n, w):
+        add("v", lambda e: e.memset(out, v), (), w, (), vc(n))
+
+    def scan(out, a, b, init, o0, o1, n, r, w, x=()):
+        add("v", lambda e: e.tensor_tensor_scan(out, a, b, init, o0, o1), r, w, x, vc(n))
+
+    def act(out, a, n, r, w, x=(), fn=ACT.Identity, **kw):
+        add("s", lambda e: e.activation(out, a, fn, **kw), r, w, x, 65.0 + 1.04 * max(64.0, n))
+
+    def mm(out, lt, rh, st, sp, n, r, bank):
+        add("p", lambda e: e.matmul(out, lt, rh, st, sp), r, [bank], (), 0.75 * max(64.0, n), 60.0)
+
+    def iota(out, pat, base, cm, n, w, flag=True):
+        if flag:
+            add("g", lambda e: e.iota(out, pat, base, cm, allow_small_or_imprecise_dtypes=True), (), w, (), 150.0 + 2.1 * n)
+        else:
+            add("g", lambda e: e.iota(out, pat, base, cm), (), w, (), 150.0 + 2.1 * n)
+
+    def gather(q, out, win, off, n, r, w, scale=None):
+        if q == "s":
+            add("s", lambda e: e.activation(out, win.indirect(off), ACT.Identity, scale=scale or 1.0), r, w, (), 70.0 + 1.62 * n)
+        elif scale:
+            add("v", lambda e: e.tensor_scalar(out, win.indirect(off), scale, None, ALU.mult), r, w, (), 55.0 + 1.62 * n)
+        else:
+            add("v", lambda e: e.tensor_copy(out, win.indirect(off)), r, w, (), 55.0 + 1.62 * n)
+
+    def dma(q, out, a, sem, r, w, lat=0.0):
+        add(q, lambda e: e.dma_start(out, a).then_inc(T.sem[sem], 16), r, w, (), 60.0, lat, "none")
+
+    def event(sem, v, r, w, lat):
+        add(None, None, r, w, (), 0.0, lat, (sem, v))
+
+    order = peers(T, topo, me)
+    back = [peers(T, topo, r).index(me) for r in order]
+    dto = [(me - r) % N for r in order]
+    dfrom = [(r - me) % N for r in order]
+    sent, got = [0], {}
+
+    def send(ls, outs, ins, sem, rd, w, nb):
+        trs = []
+        for l, o, a in zip(ls, outs, ins):
+            en = engines_for(T, topo, me, order[l])
+            share = [x for x in ls if engines_for(T, topo, me, order[x]) == en]
+            k = len(en) // len(share)
+            while k & (k - 1):
+                k -= 1
+            mine = en[share.index(l) * k:(share.index(l) + 1) * k]
+            ad = topo.addr(T.cores[order[l]])
+            trs.append((o, a, ad, sum([1 << x for x in mine])))
+            sent[0] += k
+            got[sem] = got.get(sem, 0) + k
+        s = T.sem[sem]
+        if len(trs) == 1:
+            o, a, ad, m = trs[0]
+            add("g", lambda e: e.remote_dma(o, a, s, T.sem.ls, ad[1], ad[0], m), rd, [w + "i"], (), CFG["send"],
+                CFG["lat"], "none")
+        else:
+            tr = [RemoteDMATransfer(dst_ids=[DstId(rid=ad[0], pnc=ad[1])], dma_engine_mask=m, remote_sem=s, src=a, dst=o)
+                  for o, a, ad, m in trs]
+            add("g", lambda e: e.remote_dma_fused(tr, local_sem=T.sem.ls), rd, [w + "i"], (), CFG["send"],
+                CFG["lat"], "none")
+        far = len([l for l in ls if topo.chip(T.cores[order[l]]) != topo.chip(T.cores[me])])
+        t = 16 * max(far, 1) * (CFG["row"] + nb / 25.0)
+        add("d" if far else None, None, [w + "i"], [w], (), t if far else 0.0, 0.0 if far else t, "none")
+
+    def exchange(out, a, sem, rd, w, lat):
+        for i, ls in enumerate(CFG["small"]):
+            send(ls, [out(l) for l in ls], [a(l) for l in ls], sem, rd, "x%s%d" % (sem, i), 64)
+        event(sem, got[sem], ["x%s%d" % (sem, i) for i in range(len(CFG["small"]))], w, lat)
+
+    col = lambda k: T.col[:, k:k + 1]
+    PC, GC, G16, W15, SN, M0, M4, MA, MB, H2 = range(10)
+    hcs = lambda k: T.hcs[:, k:k + 1]
+    seven = lambda s: [s % l for l in range(7)]
+
+    dma("s", T.cami[:], T.came[:], "ldc", (), ["l3"])
+    dma("y", T.hcr[0:8, 0:21], T.hc[:], "ldh", (), ["l1"])
+    dma("s", T.hcr[0:8, 21:22], T.had[:], "ldh", ["l3"], ["l2"])
+    dma("y", T.win[:, 0:P], T.ring[:], "ldr", ["l1"], ["l4"])
+    event("ldh", 32, ["l1", "l2"], ["hcr"], 2000.0)
+    event("ldc", 16, ["l3"], ["cami"], 2300.0)
+    event("ldr", 16, ["l4"], ["rin"], 5500.0)
+    for i in range(4):
+        act(T.win[:, 1024 * i:1024 * i + 1024], T.win[:, 1024 * i:1024 * i + 1024], 1024, ["rin"], ["ring%d" % i],
+            scale=1.0 / 256)
+
+    iota(T.pi[:, 0:1], [[0, 1]], 0, 1, 1, ["pi"], False)
+    iota(T.tg[:], [[1, 8], [0, 16]], 0, 0, 128, ["tg"])
+    iota(T.ti[:], [[1, 144]], 0, 0, 144, ["ti"])
+    iota(T.tabl[:], [[16, 7], [0, 8]], 0, 0, 56, ["tabl"])
+    iota(T.pt[:], [[16, 256]], 0, 1, 256, ["pt"])
+    for l, r in enumerate(order):
+        iota(T.tabr[:, :, 8 * l:8 * l + 8], [[128, 2], [0, 8]], TT * r, 0, 16, ["tabr%d" % l])
+    cp(col(PC), T.pi[:, 0:1], 1, ["pi"], ["pc"])
+    ts(T.pi[:, 1:2], T.pi[:, 0:1], 4, None, ALU.arith_shift_right, None, 1, ["pi"], ["gi"])
+    cp(col(GC), T.pi[:, 1:2], 1, ["gi"], ["gc"])
+    ts(col(G16), T.pi[:, 1:2], 16.0, None, ALU.mult, None, 1, ["gi"], ["g16"])
+    ts(col(W15), T.pi[:, 1:2], 16.0, 15.0, ALU.mult, ALU.add, 1, ["gi"], ["w15"])
+    ts(col(SN), col(PC), col(W15), None, ALU.not_equal, None, 1, ["pc", "w15"], ["sn"])
+    ts(T.gt[0:8, :], T.tg[0:8, :], T.col[0:8, PC:PC + 1], None, ALU.is_equal, None, 128, ["tg", "pc"], ["gt"])
+    ts(T.idb[:], T.ti[:, 0:128], col(PC), None, ALU.is_equal, None, 64, ["ti", "pc"], ["idb"])
+    ts(T.idh[:], T.ti[:, 0:128], col(PC), None, ALU.is_equal, None, 64, ["ti", "pc"], ["idh"])
+    ts(T.wm[:], T.ti[:], col(W15), None, ALU.is_equal, None, 72, ["ti", "w15"], ["wm"])
+    ts(T.bo[:], T.tg[:], col(GC), None, ALU.is_equal, None, 64, ["tg", "gc"], ["bo"])
+    ms(T.msk[:], 1.0, 56, ["msk"])
+    ms(T.msk[:, 0:112:16], 0.0, 7, ["msk"])
+    ms(T.zb[:], 0.0, 28, ["zb"])
+    ms(T.zf[:], 0.0, 24, ["zf"])
+    ts(T.gm[:], T.ti[:, 0:8], col(GC), None, ALU.is_equal, None, 8, ["ti", "gc"], ["gm"])
+    ts(T.r1[:], T.ti[:, 0:8], col(GC), col(SN), ALU.is_equal, ALU.mult, 8, ["ti", "gc", "sn"], ["r1"])
+    act(T.r16[:], T.r1[:], 8, ["r1"], ["r16"], scale=16.0)
+    act(T.r8[:], T.r1[:], 8, ["r1"], ["r8"], scale=8.0)
+    act(T.rh[:], T.r1[:], 8, ["r1"], ["rh"], scale=0.5)
+    act(T.wh[:], T.wm[:], 144, ["wm"], ["wh"], scale=0.5)
+    act(T.nid[:], T.idb[:], 128, ["idb"], ["nid"], scale=-1.0)
+    act(T.nbo[:], T.bo[:], 128, ["bo"], ["nbo"], scale=-1.0)
+    add("g", lambda e: e.affine_select(T.lt[:], T.nbo[:], [[-1, 128]], ALU.is_gt, 0.0, 0, 1), ["nbo"], ["lt"], (), 450.0)
+    for l in range(7):
+        act(T.i896[:, 128 * l:128 * l + 128], T.ti[:, 0:128], 128, ["ti"], ["i896_%d" % l])
+
+    tag[0] = "hc"
+    cp(T.hcf[0:8, 0:22], T.hcr[0:8, 0:22], 22, ["hcr"], ["hcf"])
+    mm(T.pq[:, 0:22], T.gt[0:8, :], T.hcf[0:8, 0:22], True, True, 256, ["gt", "hcf"], "pq")
+    cp(T.hcs[:, 0:22], T.pq[:, 0:22], 22, (), ["hcs"], ["pq"])
+    ts(T.cc[:, 0:1], hcs(21), float(P), None, ALU.min, None, 1, ["hcs"], ["cc0"])
+    for k in range(3):
+        act(T.dg[:, k, :], T.idb[:], 128, ["idb", "hcs"], ["dg%d" % k], scale=hcs(18 + k))
+
+    def hashes(e, l0, l1, xs, xr, xx, bank):
+        tag[0] = "hash%d_%d" % (e, l0)
+        ha, hb = T["ha%d" % e], T["hb%d" % e]
+        n, c0 = (l1 - l0) * 24, l0 * 24
+        ka, kb = "ha%d_%d" % (e, l0), "hb%d_%d" % (e, l0)
+        a, b, pq = ha[:, l0:l1], hb[:, l0:l1], T[bank][:, 0:n]
+        kk = [ka + "k%d" % k for k in range(3)]
+        for k in range(3):
+            ts(ha[:, l0:l1, k, :], xs, hcs(6 * e + k), hcs(6 * e + 3 + k), ALU.mult, ALU.add, n / 3, ["hcs"] + xr, [kk[k]], xx)
+        ts(b, a, P - 1, None, ALU.bitwise_and, None, n, kk, [kb])
+        ts(pq, b, 2.0, float(P - 1), ALU.mult, ALU.subtract, n, [kb], [bank])
+        tt(a, b, pq, ALU.mult, n, [kb], [ka] + kk, [bank])
+        ts(b, a, P - 1, None, ALU.bitwise_and, None, n, [ka], [kb])
+        if e == 0:
+            ts(a, b, T.cc[:, 0:1], None, ALU.mult, None, n, [kb, "cc0"], [ka])
+            ts(b, a, 12, None, ALU.arith_shift_right, None, n, [ka], [kb])
+            cp(T.off0[:, c0:c0 + n], b, n, [kb], ["off0_%d" % l for l in range(l0, l1)])
+        else:
+            ts(a, b, T.cc[:, e:e + 1], col(M4), ALU.mult, ALU.subtract, n, [kb, "cc12", "m4"], [ka])
+            ts(b, a, 12, P - 1, ALU.arith_shift_right, ALU.bitwise_and, n, [ka], [kb])
+            translate(e, b, kb, n, bank)
+
+    def translate(e, j, kj, n, bank):
+        L, tag[0] = 7 * e, "tr%d" % e
+        s0, m0 = 168 * (e - 1), 168 * (e // 3)
+        jh, acc, kh = T.jh[:, s0:s0 + n], T[bank][:, 0:n], "jh%d" % e
+        ts(jh, j, 2048.0, None, ALU.subtract, None, n, [kj], [kh])
+        mm(acc, T.idh[:], jh, True, False, n, ["idh", kh], bank)
+        steps = [(T.bq[:, i:i + 1], T.dl[:, i:i + 1]) for i in range(L - 1)]
+        steps += [(T.bq[:, L - 1:L], T.dja[:, e - 1:e]), (T.bq[:, L - 1:L], T.djb[:, e - 1:e]), (T.b2[:, e - 1:e], -float(P))]
+        for i, (b, d) in enumerate(steps):
+            km = "mk%d_%d" % (i, m0)
+            ts(T.mk[:, i, m0:m0 + n], jh, b, d, ALU.is_ge, ALU.mult, n / 2, [kh, "bq", "dl", "dja", "djb", "b2"], [km])
+            mm(acc, T.idb[:], T.mk[:, i, m0:m0 + n], False, i == len(steps) - 1, n, ["idb", km], bank)
+        ts(T["off%d" % e][:], acc, float(P + 2048), None, ALU.add, None, n, (), ["off%d" % e], [bank])
+
+    def rows(out, win, off, b, r, w):
+        add("v", lambda e: e.tensor_tensor(out, win.indirect(off), b, ALU.is_le), r, w, (), 55.0 + 1.62 * 448)
+
+    def select(z, sv, fv, ks, kf, ba, bb, bx):
+        u, tag[0] = CFG["sel"][z], "sel%d" % z
+        v = u == "v"
+        cm, c2, A, B, X = (T.cm if v else T.cn), (T.c2 if v else T.c3), T[ba], T[bb], T[bx]
+        ct, pw, of1 = T.ct[0:112, 8 * z:8 * z + 8], T.pw[:, 112 * z:112 * z + 112], T.of1[:, 56 * z:56 * z + 56]
+        mm(A[0:112, 112:120], sv, T.gm[:], True, True, 8, ["gm"] + ks, ba)
+        act(ct, A[0:112, 112:120], 8, (), ["ct%d" % z], [ba], scale=1.0 if v else -1.0, bias=0.0 if v else 0.5)
+        mm(B[:, 0:112], T.bo[:], sv, True, False, 112, ["bo"] + ks, bb)
+        mm(B[:, 0:112], T.lt[:], fv, False, True, 112, ["lt"] + kf, bb)
+        act(pw, B[:, 0:112], 112, (), ["pw%d" % z], [bb])
+        kc = [u + "cm_%d" % a for a in range(8)]
+        for a in range(8):
+            c = T.ct[0:112, 8 * z + a:8 * z + a + 1]
+            if v:
+                ts(cm[0:112, :, a, :], T.ti[0:112, 0:128], c, None, ALU.is_ge, None, 64, ["ti", "ct%d" % z], [kc[a]])
+            else:
+                act(cm[0:112, :, a, :], T.ti[0:112, 0:128], 128, ["ti", "ct%d" % z], [kc[a]], fn=ACT.Sign, bias=c)
+        mm(A[:, 128:184], T.idb[:], T.tabl[:], True, False, 56, ["idb", "tabl"], ba)
+        for a in range(8):
+            mm(A[:, 128 + a:184:8], cm[0:112, a], (T.r1 if v else T.rh)[0:112, 0:7], False, a == 7, 7, kc + ["r1", "rh"], ba)
+        ts(of1, A[:, 128:184], 0.0 if v else 7.5, None, ALU.add, None, 56, (), ["of1%d" % z], [ba])
+        if z == 0:
+            mm(X[:, 0:56], T.idb[:], T.zb[:], True, False, 56, ["idb", "zb"], bx)
+        else:
+            mm(X[:, 0:56], T.idb[:], T.tabr[:, 0 if v else 1, :], True, False, 56, ["idb"] + seven("tabr%d"), bx)
+        for a in range(8):
+            mm(X[:, a:56:8], cm[0:112, a], (T.r16 if v else T.r8)[0:112, 0:7], False, False, 7, kc + ["r16", "r8"], bx)
+        bd = (bb, ba)
+        for h in range(2):
+            c0, D, oh = 448 * h, T[bd[h]][:, 0:448], T.of1[:, 56 * z + 28 * h:56 * z + 28 * h + 28]
+            if v:
+                rows(c2[:, c0:c0 + 448], pw, oh, T.i896[:, c0:c0 + 448], ["pw%d" % z, "of1%d" % z] + seven("i896_%d"),
+                     ["vc2_%d" % h])
+            else:
+                gather("s", T.g2[:, c0:c0 + 448], pw, oh, 448, ["pw%d" % z, "of1%d" % z], ["g2_%d" % h])
+                mm(D, T.idb[:], T.i896[:, c0:c0 + 448], True, False, 448, ["idb"] + seven("i896_%d"), bd[h])
+                mm(D, T.nid[:], T.g2[:, c0:c0 + 448], False, True, 448, ["nid", "g2_%d" % h], bd[h])
+                act(c2[:, c0:c0 + 448], D, 448, (), ["sc2_%d" % h], [bd[h]], fn=ACT.Sign, bias=0.5)
+        for s in range(16):
+            mm(X[:, 0:56], (T.wm if v else T.wh)[:, 15 - s:143 - s], c2[:, s:896:16], False, s == 15, 56,
+               ["wm", "wh", u + "c2_0", u + "c2_1"], bx)
+        if z == 0:
+            ts(T.tl[:], X[:, 0:56], TT * me + (0.0 if v else 128.0), None, ALU.add, None, 56, (), ["tl"], [bx])
+
+    def packets(e, wkeys):
+        n, first = CAP, len(ops)
+        ga, ou, off = T["ga%d" % e], T["ou%d" % e], T["off%d" % e]
+        win = T.win[:, 0:P + 896 * e]
+        for l in range(7):
+            nv, tag[0] = CFG["nv"][e][l], "ga%d_%d" % (e, l)
+            for q, k0, k1 in (("v", 0, nv), ("s", nv, 3)):
+                if k1 > k0:
+                    gather(q, ga[:, (3 * l + k0) * n:(3 * l + k1) * n], win, off[:, (3 * l + k0) * 8:(3 * l + k1) * 8],
+                           (k1 - k0) * n, wkeys + ["off0_%d" % l if e == 0 else "off%d" % e],
+                           ["ga%d_%d_%d" % (e, l, k) for k in range(k0, k1)])
+            bank, tag[0] = "pd%d" % (l % 4), "oq%d_%d" % (e, l)
+            ps = T[bank][:, 0:n]
+            for k in range(3):
+                mm(ps, T.dg[:, k, :], ga[:, (3 * l + k) * n:(3 * l + k + 1) * n], k == 0, k == 2, n,
+                   ["dg%d" % k, "ga%d_%d_%d" % (e, l, k)], bank)
+            qq = T.qq[:, l * n:l * n + n]
+            ts(qq, ps, 127.5 / 256, None, ALU.subtract, None, n, (), ["qq%d" % l], [bank])
+            tag[0] = "ou%d_%d" % (e, l)
+            tt(ou[:, l * n:(l + 1) * n], ps, qq, ALU.subtract, n, ["qq%d" % l], ["ou%d_%d" % (e, l)], [bank])
+        for i, ls in enumerate(CFG["calls"]):
+            tag[0] = "ou%d_%d" % (e, max(ls))
+            send(ls, [T.win[:, P + 896 * e + (dto[l] - 1) * n:P + 896 * e + dto[l] * n] for l in ls],
+                 [ou[:, l * n:(l + 1) * n] for l in ls], "a%d" % e, ["ou%d_%d" % (e, l) for l in ls], "s%d_%d" % (e, i), 2 * n)
+        for q in "vs":
+            mine, last = [i for i in range(first, len(ops)) if ops[i]["q"] == q], None
+            for w in CFG["c" + q].split():
+                for i in [i for i in mine if ops[i]["tag"] == "%s%d_%s" % ({"g": "ga", "q": "oq", "o": "ou"}[w[0]], e, w[1])]:
+                    if last is not None:
+                        ops[i]["ord"].append(last)
+                    last = i
+        event("a%d" % e, got["a%d" % e], ["s%d_%d" % (e, i) for i in range(len(CFG["calls"]))], ["log%d" % e], 200.0)
+
+    tag[0] = "flags"
+    for e in range(3):
+        c = slice(112 * e, 112 * e + 112)
+        cp(T.fo[:, c], T.cami[:, e], 112, ["cami"], ["fo%d" % e])
+        scan(T.so[:, c], T.msk[:], T.fo[:, c], 0.0, ALU.mult, ALU.add, 56, ["fo%d" % e, "msk"], ["so%d" % e])
+        if e:
+            act(T.fs[:, :, e - 1, :], T.fo[:, c], 112, ["fo%d" % e], ["fs%d" % e])
+    exchange(lambda l: T.fr[:, back[l]], lambda l: T.fs[:, dfrom[l] - 1], "fl", ["fs1", "fs2"], ["fr"], CFG["first"])
+    select(0, T.so[:, 0:112], T.fo[:, 0:112], ["so0"], ["fo0"], "pa", "pb", "px")
+    exchange(lambda l: T.xl[:, back[l]], lambda l: T.tl[:, 8 * (dfrom[l] - 1):8 * dfrom[l]], "li", ["tl"], ["xl"], 200.0)
+    tag[0] = "cnt"
+    mm(T.pq[:, 32:53], T.bo[:], T.so[:, 15:336:16], True, True, 21, ["bo", "so0", "so1", "so2"], "pq")
+    scan(T.bq[:, 0:21], T.pq[:, 32:53], T.zf[:, 0:21], -2048.0, ALU.add, ALU.add, 21, ["zf"], ["bq"], ["pq"])
+    ts(T.dl[:, 0:21], T.pq[:, 32:53], -1.0, float(CAP), ALU.mult, ALU.add, 21, (), ["dl"], ["pq"])
+    scan(T.cd[:, 0:21], T.dl[:, 0:21], T.zf[:, 0:21], 0.0, ALU.add, ALU.add, 21, ["zf", "dl"], ["cd"])
+    cp(T.pi[:, 2:3], hcs(21), 1, ["hcs"], ["mi"])
+    ts(T.pi[:, 3:4], T.pi[:, 2:3], P - 1, None, ALU.bitwise_and, None, 1, ["mi"], ["mj"])
+    ts(col(M4), T.pi[:, 3:4], float(P), None, ALU.mult, None, 1, ["mj"], ["m4"])
+    ts(col(MA), T.pi[:, 3:4], float(P), None, ALU.subtract, None, 1, ["mj"], ["ma"])
+    ts(col(MB), T.pi[:, 3:4], -1.0, 2048.0, ALU.mult, ALU.add, 1, ["mj"], ["mb"])
+    ts(col(M0), T.pi[:, 3:4], col(G16), None, ALU.add, None, 1, ["mj", "g16"], ["m0"])
+    ts(col(H2), hcs(21), 2048.0, None, ALU.add, None, 1, ["hcs"], ["h2"])
+    ts(T.dj[:, 0:3], T.cd[:, 5:21:7], -1.0, col(MA), ALU.mult, ALU.add, 3, ["cd", "ma"], ["dj"])
+    cp(T.djr[:, 0:3], T.dj[:, 0:3], 3, ["dj"], ["djr"])
+    act(T.dja[:, 0:3], T.djr[:, 0:3], 3, ["djr"], ["dja"])
+    tt(T.djb[:, 0:3], T.dj[:, 0:3], T.djr[:, 0:3], ALU.subtract, 6, ["dj", "djr"], ["djb"])
+    ts(T.b2[:, 0:3], T.bq[:, 6:21:7], col(MB), None, ALU.max, None, 3, ["bq", "mb"], ["b2"])
+    ts(T.cc[:, 1:3], T.bq[:, 6:14:7], col(H2), float(P), ALU.add, ALU.min, 2, ["bq", "h2"], ["cc12"])
+    ts(T.nw[:, 0:1], T.bq[:, 20:21], col(H2), None, ALU.add, None, 1, ["bq", "h2"], ["nw"])
+    dma("y", T.now[:], T.nw[0:128:16, 0:1], "sty", ["nw"], ["now"], 2000.0)
+
+    def select_sent(e, ba, bb, bx):
+        tag[0] = "sel%d" % e
+        c = slice(112 * e - 112, 112 * e)
+        act(T.fq[:, c], T.fr[:, :, e - 1, :], 112, ["fr"], ["fq%d" % e])
+        scan(T.sr[:, c], T.msk[:], T.fq[:, c], 0.0, ALU.mult, ALU.add, 56, ["fq%d" % e, "msk"], ["sr%d" % e])
+        select(e, T.sr[:, c], T.fq[:, c], ["sr%d" % e], ["fq%d" % e], ba, bb, bx)
+
+    hashes(0, 0, 4, T.xl[:, 0:4], ["xl"], [], "pd0")
+    hashes(0, 4, 7, T.xl[:, 4:7], ["xl"], [], "pd1")
+    tag[0] = "last"
+    ts(T.ja[:], T.pt[:], col(M0), None, ALU.subtract, None, 256, ["pt", "m0", "tl"], ["ja"])
+    ts(T.jb[:], T.ja[:], P - 1, None, ALU.bitwise_and, None, 256, ["ja"], ["jb"])
+    translate(3, T.jb[:], "jb", 256, "pq")
+    select_sent(1, "pa", "pb", "px")
+    hashes(1, 0, 7, T.px[:, 0:56], [], ["px"], "pa")
+    select_sent(2, "pb", "pb", "px")
+    hashes(2, 0, 7, T.px[:, 0:56], [], ["px"], "pa")
+    logs = ["ring0", "ring1", "ring2", "ring3", "log0", "log1", "log2"]
+    for e in range(3):
+        packets(e, logs[:4 + e])
+    tag[0] = "out"
+    for i, (c0, c1, q) in enumerate(CFG["ych"]):
+        gather(q, T.yb[:, c0:c1], T.win[:], T.off3[:, c0 // 16:c1 // 16], c1 - c0, logs + ["off3"], ["yb%d" % i], 256.0)
+        dma("y", T.y[:, c0:c1], T.yb[:, c0:c1], "sty", ["yb%d" % i], ["st%d" % i], 2000.0 + 1.6 * (P - c0))
+    tail = [(s, got[s]) for s in got]
+    tail += [("ldh", 32), ("ldc", 16), ("ldr", 16), ("ls", sent[0]), ("sty", 16 * (len(CFG["ych"]) + 1))]
+    return ops, tail
+
+
+def rank_program(g, core, T, topo):
+    me = T.rank_of(core)
+    if me is None:
+        return
+    ops, tail = build(T, topo, me)
+    if "order" not in CFG:
+        CFG["order"] = plan(ops)
+    emit(g, T, ops, CFG["order"], tail)

@@ -8,13 +8,13 @@ ACT = ActivationFunctionType
 F32, BF, I32, U16, F16 = "float32", "bfloat16", "int32", "uint16", "float16"
 CFG = {
     "sel": ("v", "v", "s"),
-    "nv": ((1, 1, 1, 0, 1, 0, 0), (1, 1, 1, 0, 1, 0, 0), (1, 2, 1, 0, 1, 1, 1)),
+    "nv": ((1, 1, 1, 0, 1, 0, 0), (1, 1, 0, 0, 0, 0, 0), (1, 2, 1, 0, 1, 1, 1)),
     "calls": ((0,), (1,), (2,), (3,), (4,), (5,), (6,)),
     "small": ((0, 1, 6), (2, 3), (4, 5)),
     "cv": "g0 g1 g2 q0 o0 q1 g3 g4 o1 q2 g5 o2 q3 g6 o3 q4 q5 o4 o5 q6 o6", "cs": "g0 g1 g2 g3 g4 g5 g6",
-    "ych": ((0, 256, "s"), (256, 512, "v"), (512, 1024, "s"), (1024, 1536, "v"), (1536, 2048, "s"),
-            (2048, 2560, "v"), (2560, 3072, "s"), (3072, 3584, "v"), (3584, 4096, "s")),
-    "send": 300.0, "lat": 1600.0, "row": 20.0, "first": 2000.0, "tries": 1500, "seed": 1,
+    "ych": ((0, 128, "s"), (128, 256, "v"), (256, 640, "s"), (640, 1024, "v"), (1024, 1536, "s"), (1536, 2048, "v"),
+            (2048, 2560, "s"), (2560, 3072, "v"), (3072, 3584, "s"), (3584, 4096, "v")),
+    "send": 300.0, "lat": 900.0, "row": 15.0, "first": 1500.0, "tries": 1500, "seed": 1,
 }
 
 
@@ -26,9 +26,8 @@ SCRATCH = {
     "win": sb([P + 3 * 896], BF), "yb": sb([P], F32),
     "ga0": sb([21 * CAP], BF), "ga1": sb([21 * CAP], BF), "ga2": sb([21 * CAP], BF),
     "qq": sb([896], I32), "ou0": sb([896], BF), "ou1": sb([896], BF), "ou2": sb([896], BF),
-    "hcr": sb([24], I32), "hcf": sb([24], F32), "hcs": sb([24], F32), "cami": sb([3, 7, 16], I32),
-    "fo": sb([336], BF), "so": sb([336], BF), "fs": sb([7, 2, 16], BF), "fr": sb([7, 2, 16], BF),
-    "fq": sb([224], BF), "sr": sb([224], BF),
+    "hcr": sb([24], I32), "hcf": sb([24], F32), "hcs": sb([24], F32), "cami": sb([336], I32),
+    "fo": sb([336], BF), "so": sb([336], BF), "fr": sb([112], BF), "sr": sb([112], BF),
     "msk": sb([112], BF), "pi": sb([4], I32), "col": sb([16], F32),
     "ti": sb([144], BF), "tg": sb([128], BF), "tabr": sb([2, 56], BF), "tabl": sb([56], BF), "zb": sb([56], BF),
     "zf": sb([24], F32), "i896": sb([896], BF), "pt": sb([256], F32), "gt": sb([128], F32),
@@ -39,7 +38,7 @@ SCRATCH = {
     "dja": sb([4], F32), "djb": sb([4], F32), "b2": sb([4], F32), "cc": sb([4], F32), "nw": sb([4], F32),
     "ct": sb([24], F32), "pw": sb([336], BF), "cm": sb([8, 8, 16], BF), "cn": sb([8, 8, 16], BF),
     "of1": sb([168], U16), "c2": sb([896], BF), "c3": sb([896], BF), "g2": sb([896], BF),
-    "tl": sb([56], U16), "xl": sb([7, 8], U16),
+    "tl": sb([112], U16), "xl": sb([112], U16),
     "ha0": sb([7, 3, 8], I32), "hb0": sb([7, 3, 8], I32), "ha1": sb([7, 3, 8], I32), "hb1": sb([7, 3, 8], I32),
     "ha2": sb([7, 3, 8], I32), "hb2": sb([7, 3, 8], I32),
     "off0": sb([168], U16), "off1": sb([168], U16), "off2": sb([168], U16), "off3": sb([256], U16),
@@ -47,7 +46,7 @@ SCRATCH = {
 }
 for _b in ("pd0", "pd1", "pd2", "pd3", "pa", "pb", "px", "pq"):
     SCRATCH[_b] = ("psum", [128, 512], F32)
-SEMAPHORES = ["cv", "cs", "cp", "cg", "ldh", "ldc", "ldr", "sty", "ls", "fl", "li", "a0", "a1", "a2"]
+SEMAPHORES = ["cv", "cs", "cp", "cg", "ldh", "ldc", "ldd", "ldr", "sty", "ls", "fl", "li0", "li1", "a0", "a1", "a2"]
 CNT = {"v": "cv", "s": "cs", "p": "cp", "g": "cg"}
 SYNC = 110.0
 
@@ -112,7 +111,7 @@ def one_pass(ops, before, after, pr):
 def rank_of_part(t):
     if t[:2] in ("ga", "ou", "oq") and t != "out":
         return (4.0, 7.0, 9.0)[int(t[2])]
-    return {"sel0": 1.0, "cnt": 2.0, "sel1": 5.0, "sel2": 5.5, "hash1_0": 6.0, "tr1": 6.0, "hash2_0": 8.0, "tr2": 8.0,
+    return {"sel0": 1.0, "cnt": 2.0, "sel1": 1.5, "sel2": 3.0, "hash1_0": 6.0, "tr1": 6.0, "hash2_0": 8.0, "tr2": 8.0,
             "last": 8.5, "tr3": 8.5, "out": 10.0, "hash0_0": 0.5, "hash0_4": 0.6}.get(t, 0.0)
 
 
@@ -326,7 +325,7 @@ def build(T, topo, me):
 
     def exchange(out, a, sem, rd, w, lat):
         for i, ls in enumerate(CFG["small"]):
-            send(ls, [out(l) for l in ls], [a(l) for l in ls], sem, rd, "x%s%d" % (sem, i), 64)
+            send(ls, [out(l) for l in ls], [a(l) for l in ls], sem, rd, "x%s%d" % (sem, i), 32)
         event(sem, got[sem], ["x%s%d" % (sem, i) for i in range(len(CFG["small"]))], w, lat)
 
     col = lambda k: T.col[:, k:k + 1]
@@ -334,12 +333,14 @@ def build(T, topo, me):
     hcs = lambda k: T.hcs[:, k:k + 1]
     seven = lambda s: [s % l for l in range(7)]
 
-    dma("s", T.cami[:], T.came[:], "ldc", (), ["l3"])
-    dma("y", T.hcr[0:8, 0:21], T.hc[:], "ldh", (), ["l1"])
+    dma("y", T.cami[:, 0:112], T.came[:, 0:112], "ldc", (), ["l0"])
+    dma("s", T.cami[:, 112:336], T.came[:, 112:336], "ldd", (), ["l3"])
+    dma("y", T.hcr[0:8, 0:21], T.hc[:], "ldh", ["l0"], ["l1"])
     dma("s", T.hcr[0:8, 21:22], T.had[:], "ldh", ["l3"], ["l2"])
     dma("y", T.win[:, 0:P], T.ring[:], "ldr", ["l1"], ["l4"])
-    event("ldh", 32, ["l1", "l2"], ["hcr"], 2000.0)
-    event("ldc", 16, ["l3"], ["cami"], 2300.0)
+    event("ldh", 32, ["l1", "l2"], ["hcr"], 2100.0)
+    event("ldc", 16, ["l0"], ["cami0"], 2100.0)
+    event("ldd", 16, ["l3"], ["cami1", "cami2"], 2300.0)
     event("ldr", 16, ["l4"], ["rin"], 5500.0)
     for i in range(4):
         act(T.win[:, 1024 * i:1024 * i + 1024], T.win[:, 1024 * i:1024 * i + 1024], 1024, ["rin"], ["ring%d" % i],
@@ -383,7 +384,7 @@ def build(T, topo, me):
     cp(T.hcf[0:8, 0:22], T.hcr[0:8, 0:22], 22, ["hcr"], ["hcf"])
     mm(T.pq[:, 0:22], T.gt[0:8, :], T.hcf[0:8, 0:22], True, True, 256, ["gt", "hcf"], "pq")
     cp(T.hcs[:, 0:22], T.pq[:, 0:22], 22, (), ["hcs"], ["pq"])
-    ts(T.cc[:, 0:1], hcs(21), float(P), None, ALU.min, None, 1, ["hcs"], ["cc0"])
+    ts(T.cc[:, 0:1], hcs(21), float(P), 1.0 / P, ALU.min, ALU.mult, 1, ["hcs"], ["cc0"])
     for k in range(3):
         act(T.dg[:, k, :], T.idb[:], 128, ["idb", "hcs"], ["dg%d" % k], scale=hcs(18 + k))
 
@@ -401,9 +402,8 @@ def build(T, topo, me):
         tt(a, b, pq, ALU.mult, n, [kb], [ka] + kk, [bank])
         ts(b, a, P - 1, None, ALU.bitwise_and, None, n, [ka], [kb])
         if e == 0:
-            ts(a, b, T.cc[:, 0:1], None, ALU.mult, None, n, [kb, "cc0"], [ka])
-            ts(b, a, 12, None, ALU.arith_shift_right, None, n, [ka], [kb])
-            cp(T.off0[:, c0:c0 + n], b, n, [kb], ["off0_%d" % l for l in range(l0, l1)])
+            ts(a, b, T.cc[:, 0:1], 2047.5 - 2.0 ** -13, ALU.mult, ALU.subtract, n, [kb, "cc0"], [ka])
+            ts(T.off0[:, c0:c0 + n], a, 2047.0, None, ALU.add, None, n, [ka], ["off0_%d" % l for l in range(l0, l1)])
         else:
             ts(a, b, T.cc[:, e:e + 1], col(M4), ALU.mult, ALU.subtract, n, [kb, "cc12", "m4"], [ka])
             ts(b, a, 12, P - 1, ALU.arith_shift_right, ALU.bitwise_and, n, [ka], [kb])
@@ -431,23 +431,25 @@ def build(T, topo, me):
         v = u == "v"
         cm, c2, A, B, X = (T.cm if v else T.cn), (T.c2 if v else T.c3), T[ba], T[bb], T[bx]
         ct, pw, of1 = T.ct[0:112, 8 * z:8 * z + 8], T.pw[:, 112 * z:112 * z + 112], T.of1[:, 56 * z:56 * z + 56]
-        mm(A[0:112, 112:120], sv, T.gm[:], True, True, 8, ["gm"] + ks, ba)
-        act(ct, A[0:112, 112:120], 8, (), ["ct%d" % z], [ba], scale=1.0 if v else -1.0, bias=0.0 if v else 0.5)
         mm(B[:, 0:112], T.bo[:], sv, True, False, 112, ["bo"] + ks, bb)
         mm(B[:, 0:112], T.lt[:], fv, False, True, 112, ["lt"] + kf, bb)
         act(pw, B[:, 0:112], 112, (), ["pw%d" % z], [bb])
+        mm(A[0:112, 112:120], sv, T.gm[:], True, True, 8, ["gm"] + ks, ba)
+        if not v:
+            act(ct, A[0:112, 112:120], 8, (), ["ct%d" % z], [ba], scale=-1.0, bias=0.5)
         kc = [u + "cm_%d" % a for a in range(8)]
         for a in range(8):
-            c = T.ct[0:112, 8 * z + a:8 * z + a + 1]
             if v:
-                ts(cm[0:112, :, a, :], T.ti[0:112, 0:128], c, None, ALU.is_ge, None, 64, ["ti", "ct%d" % z], [kc[a]])
+                ts(cm[0:112, :, a, :], T.ti[0:112, 0:128], A[0:112, 112 + a:113 + a], None, ALU.is_ge, None, 64, ["ti"],
+                   [kc[a]], [ba])
             else:
-                act(cm[0:112, :, a, :], T.ti[0:112, 0:128], 128, ["ti", "ct%d" % z], [kc[a]], fn=ACT.Sign, bias=c)
+                act(cm[0:112, :, a, :], T.ti[0:112, 0:128], 128, ["ti", "ct%d" % z], [kc[a]], fn=ACT.Sign,
+                    bias=T.ct[0:112, 8 * z + a:8 * z + a + 1])
         mm(A[:, 128:184], T.idb[:], T.tabl[:], True, False, 56, ["idb", "tabl"], ba)
         for a in range(8):
             mm(A[:, 128 + a:184:8], cm[0:112, a], (T.r1 if v else T.rh)[0:112, 0:7], False, a == 7, 7, kc + ["r1", "rh"], ba)
         ts(of1, A[:, 128:184], 0.0 if v else 7.5, None, ALU.add, None, 56, (), ["of1%d" % z], [ba])
-        if z == 0:
+        if z < 2:
             mm(X[:, 0:56], T.idb[:], T.zb[:], True, False, 56, ["idb", "zb"], bx)
         else:
             mm(X[:, 0:56], T.idb[:], T.tabr[:, 0 if v else 1, :], True, False, 56, ["idb"] + seven("tabr%d"), bx)
@@ -467,8 +469,11 @@ def build(T, topo, me):
         for s in range(16):
             mm(X[:, 0:56], (T.wm if v else T.wh)[:, 15 - s:143 - s], c2[:, s:896:16], False, s == 15, 56,
                ["wm", "wh", u + "c2_0", u + "c2_1"], bx)
-        if z == 0:
-            ts(T.tl[:], X[:, 0:56], TT * me + (0.0 if v else 128.0), None, ALU.add, None, 56, (), ["tl"], [bx])
+        if z < 2:
+            c = 56 * z
+            ts(T.tl[:, c:c + 56], X[:, 0:56], TT * me + (0.0 if v else 128.0), None, ALU.add, None, 56, (), ["tl%d" % z], [bx])
+            exchange(lambda l: T.xl[:, c + 8 * back[l]:c + 8 * back[l] + 8],
+                     lambda l: T.tl[:, c + 8 * dfrom[l] - 8:c + 8 * dfrom[l]], "li%d" % z, ["tl%d" % z], ["xl%d" % z], 200.0)
 
     def packets(e, wkeys):
         n, first = CAP, len(ops)
@@ -506,13 +511,12 @@ def build(T, topo, me):
     tag[0] = "flags"
     for e in range(3):
         c = slice(112 * e, 112 * e + 112)
-        cp(T.fo[:, c], T.cami[:, e], 112, ["cami"], ["fo%d" % e])
+        cp(T.fo[:, c], T.cami[:, c], 112, ["cami%d" % e], ["fo%d" % e])
         scan(T.so[:, c], T.msk[:], T.fo[:, c], 0.0, ALU.mult, ALU.add, 56, ["fo%d" % e, "msk"], ["so%d" % e])
-        if e:
-            act(T.fs[:, :, e - 1, :], T.fo[:, c], 112, ["fo%d" % e], ["fs%d" % e])
-    exchange(lambda l: T.fr[:, back[l]], lambda l: T.fs[:, dfrom[l] - 1], "fl", ["fs1", "fs2"], ["fr"], CFG["first"])
+    exchange(lambda l: T.fr[:, 16 * back[l]:16 * back[l] + 16], lambda l: T.fo[:, 208 + 16 * dfrom[l]:224 + 16 * dfrom[l]],
+             "fl", ["fo2"], ["fr"], CFG["first"])
     select(0, T.so[:, 0:112], T.fo[:, 0:112], ["so0"], ["fo0"], "pa", "pb", "px")
-    exchange(lambda l: T.xl[:, back[l]], lambda l: T.tl[:, 8 * (dfrom[l] - 1):8 * dfrom[l]], "li", ["tl"], ["xl"], 200.0)
+    select(1, T.so[:, 112:224], T.fo[:, 112:224], ["so1"], ["fo1"], "pd2", "pd2", "pd3")
     tag[0] = "cnt"
     mm(T.pq[:, 32:53], T.bo[:], T.so[:, 15:336:16], True, True, 21, ["bo", "so0", "so1", "so2"], "pq")
     scan(T.bq[:, 0:21], T.pq[:, 32:53], T.zf[:, 0:21], -2048.0, ALU.add, ALU.add, 21, ["zf"], ["bq"], ["pq"])
@@ -527,30 +531,24 @@ def build(T, topo, me):
     ts(col(H2), hcs(21), 2048.0, None, ALU.add, None, 1, ["hcs"], ["h2"])
     ts(T.dj[:, 0:3], T.cd[:, 5:21:7], -1.0, col(MA), ALU.mult, ALU.add, 3, ["cd", "ma"], ["dj"])
     cp(T.djr[:, 0:3], T.dj[:, 0:3], 3, ["dj"], ["djr"])
-    act(T.dja[:, 0:3], T.djr[:, 0:3], 3, ["djr"], ["dja"])
+    cp(T.dja[:, 0:3], T.djr[:, 0:3], 3, ["djr"], ["dja"])
     tt(T.djb[:, 0:3], T.dj[:, 0:3], T.djr[:, 0:3], ALU.subtract, 6, ["dj", "djr"], ["djb"])
     ts(T.b2[:, 0:3], T.bq[:, 6:21:7], col(MB), None, ALU.max, None, 3, ["bq", "mb"], ["b2"])
     ts(T.cc[:, 1:3], T.bq[:, 6:14:7], col(H2), float(P), ALU.add, ALU.min, 2, ["bq", "h2"], ["cc12"])
     ts(T.nw[:, 0:1], T.bq[:, 20:21], col(H2), None, ALU.add, None, 1, ["bq", "h2"], ["nw"])
     dma("y", T.now[:], T.nw[0:128:16, 0:1], "sty", ["nw"], ["now"], 2000.0)
 
-    def select_sent(e, ba, bb, bx):
-        tag[0] = "sel%d" % e
-        c = slice(112 * e - 112, 112 * e)
-        act(T.fq[:, c], T.fr[:, :, e - 1, :], 112, ["fr"], ["fq%d" % e])
-        scan(T.sr[:, c], T.msk[:], T.fq[:, c], 0.0, ALU.mult, ALU.add, 56, ["fq%d" % e, "msk"], ["sr%d" % e])
-        select(e, T.sr[:, c], T.fq[:, c], ["sr%d" % e], ["fq%d" % e], ba, bb, bx)
-
-    hashes(0, 0, 4, T.xl[:, 0:4], ["xl"], [], "pd0")
-    hashes(0, 4, 7, T.xl[:, 4:7], ["xl"], [], "pd1")
+    tag[0] = "sel2"
+    scan(T.sr[:], T.msk[:], T.fr[:], 0.0, ALU.mult, ALU.add, 56, ["fr", "msk"], ["sr"])
+    select(2, T.sr[:], T.fr[:], ["sr"], ["fr"], "pb", "pb", "pq")
+    hashes(0, 0, 4, T.xl[:, 0:32], ["xl0"], [], "pd0")
+    hashes(0, 4, 7, T.xl[:, 32:56], ["xl0"], [], "pd1")
+    hashes(1, 0, 7, T.xl[:, 56:112], ["xl1"], [], "pa")
+    hashes(2, 0, 7, T.pq[:, 0:56], [], ["pq"], "px")
     tag[0] = "last"
-    ts(T.ja[:], T.pt[:], col(M0), None, ALU.subtract, None, 256, ["pt", "m0", "tl"], ["ja"])
+    ts(T.ja[:], T.pt[:], col(M0), None, ALU.subtract, None, 256, ["pt", "m0", "tl0"], ["ja"])
     ts(T.jb[:], T.ja[:], P - 1, None, ALU.bitwise_and, None, 256, ["ja"], ["jb"])
-    translate(3, T.jb[:], "jb", 256, "pq")
-    select_sent(1, "pa", "pb", "px")
-    hashes(1, 0, 7, T.px[:, 0:56], [], ["px"], "pa")
-    select_sent(2, "pb", "pb", "px")
-    hashes(2, 0, 7, T.px[:, 0:56], [], ["px"], "pa")
+    translate(3, T.jb[:], "jb", 256, "pb")
     logs = ["ring0", "ring1", "ring2", "ring3", "log0", "log1", "log2"]
     for e in range(3):
         packets(e, logs[:4 + e])
@@ -559,7 +557,7 @@ def build(T, topo, me):
         gather(q, T.yb[:, c0:c1], T.win[:], T.off3[:, c0 // 16:c1 // 16], c1 - c0, logs + ["off3"], ["yb%d" % i], 256.0)
         dma("y", T.y[:, c0:c1], T.yb[:, c0:c1], "sty", ["yb%d" % i], ["st%d" % i], 2000.0 + 1.6 * (P - c0))
     tail = [(s, got[s]) for s in got]
-    tail += [("ldh", 32), ("ldc", 16), ("ldr", 16), ("ls", sent[0]), ("sty", 16 * (len(CFG["ych"]) + 1))]
+    tail += [("ldh", 32), ("ldc", 16), ("ldd", 16), ("ldr", 16), ("ls", sent[0]), ("sty", 16 * (len(CFG["ych"]) + 1))]
     return ops, tail
 
 

@@ -7,15 +7,29 @@ ALU = AluOpType
 ACT = ActivationFunctionType
 F32, BF, I32, U16, F16 = "float32", "bfloat16", "int32", "uint16", "float16"
 CFG = {
-    "sel": ("v", "v", "s"),
-    "nv": ((1, 1, 1, 0, 1, 0, 0), (1, 1, 0, 0, 0, 0, 0), (1, 2, 1, 0, 1, 1, 1)),
-    "calls": ((0,), (1,), (2,), (3,), (4,), (5,), (6,)),
+    "sel": (("v", "v"), ("v", "v"), ("s", "s")),
+    "pick": ("vv ssss sss vvv sss sss sss", "vv ssss sss sss sss sss sss", "vv ssss vvv sss sss sss v ss"),
+    "mod": ((((0, 1), "one"), ((2, 3), "one"), ((4,), "one"), ((5,), "two"), ((6,), "two")),) * 3,
+    "lots": ((0, 1, 2, 3), (4,), (5, 6)),
+    "up": ("sssssss",) * 3,
     "small": ((0, 1, 6), (2, 3), (4, 5)),
-    "cv": "g0 g1 g2 q0 o0 q1 g3 g4 o1 q2 g5 o2 q3 g6 o3 q4 q5 o4 o5 q6 o6", "cs": "g0 g1 g2 g3 g4 g5 g6",
-    "ych": ((0, 128, "s"), (128, 256, "v"), (256, 640, "s"), (640, 1024, "v"), (1024, 1536, "s"), (1536, 2048, "v"),
-            (2048, 2560, "s"), (2560, 3072, "v"), (3072, 3584, "s"), (3584, 4096, "v")),
-    "send": 300.0, "lat": 900.0, "row": 15.0, "first": 1500.0, "tries": 1500, "seed": 1,
+    "lists": (((0, 1), (2, 3)), ((4, 5, 6),)),
+    "scale": [],
+    "ych": ((0, 768, "s"), (768, 1536, "v"), (1536, 2176, "s"), (2176, 2816, "v"), (2816, 3200, "s"), (3200, 3584, "v"),
+            (3584, 3840, "s"), (3840, 4096, "v")),
+    "send": 300.0, "lat": 1200.0, "row": 12.0, "first": 1500.0, "tries": 22000, "seed": 3, "pe": 0.65, "sync": 110.0,
+    "fv": 48.0, "fs": 70.0, "cy": 0.88, "ga": 1.45,
+    "parts": "sel0 flags sel0a sel0b hc sel1 hash0_0 hash0_4 r0 sel2 cnt hash1_0 tr1 r1 hash2_0 tr2 r2 last tr3 out tab scale",
+    "due": {"end": 36000.0, "xfl0i": 4200, "xfl1i": 4500, "xfl2i": 4800, "tl0": 5900, "tl1": 6900, "tl2": 9800,
+            "off0_0": 10600, "off0_4": 11400, "off1": 17100, "off2": 23900},
+    "tl": "vvs", "halves": ((0, 4, "px"), (4, 7, "pd3")), "hash0": ((0, 4), (4, 7)),
+    "cases": ((1.25, 1.0, 0.9, 1.0), (1.0, 1.4, 1.3, 1.5), (1.3, 1.4, 1.2, 2.0)), "slack": 300.0,
 }
+for _e, _t in enumerate((12000, 18600, 25400)):
+    for _l in range(7):
+        CFG["due"]["s%d_%di" % (_e, _l)] = _t + 500 * _l
+QOFF = 1088.0
+MAGIC = 3.0 * 2 ** 30
 
 
 def sb(shape, d):
@@ -25,28 +39,32 @@ def sb(shape, d):
 SCRATCH = {
     "win": sb([P + 3 * 896], BF), "yb": sb([P], F32),
     "ga0": sb([21 * CAP], BF), "ga1": sb([21 * CAP], BF), "ga2": sb([21 * CAP], BF),
-    "qq": sb([896], I32), "ou0": sb([896], BF), "ou1": sb([896], BF), "ou2": sb([896], BF),
+    "qh": sb([896], F16), "qf": sb([896], F32), "ou0": sb([896], BF), "ou1": sb([896], BF), "ou2": sb([896], BF),
     "hcr": sb([24], I32), "hcf": sb([24], F32), "hcs": sb([24], F32), "cami": sb([336], I32),
-    "fo": sb([336], BF), "so": sb([336], BF), "fr": sb([112], BF), "sr": sb([112], BF),
-    "msk": sb([112], BF), "pi": sb([4], I32), "col": sb([16], F32),
-    "ti": sb([144], BF), "tg": sb([128], BF), "tabr": sb([2, 56], BF), "tabl": sb([56], BF), "zb": sb([56], BF),
-    "zf": sb([24], F32), "i896": sb([896], BF), "pt": sb([256], F32), "gt": sb([128], F32),
-    "idb": sb([128], BF), "nid": sb([128], BF), "idh": sb([128], F16), "wm": sb([144], BF), "wh": sb([144], BF),
-    "bo": sb([128], BF), "nbo": sb([128], BF), "lt": sb([128], BF), "gm": sb([8], BF),
-    "r1": sb([8], BF), "r16": sb([8], BF), "rh": sb([8], BF), "r8": sb([8], BF), "dg": sb([3, 128], BF),
+    "fo": sb([336], BF), "so": sb([352], BF), "pw0": sb([112], BF), "pwo": sb([224], BF), "pwr": sb([112], BF),
+    "msk": sb([224], BF), "pi": sb([4], I32), "col": sb([24], F32),
+    "ti": sb([144], BF), "tg": sb([128], BF), "tabr": sb([56], BF), "tab0": sb([56], BF), "tabl": sb([56], BF),
+    "tabx": sb([56], BF), "half": sb([256], BF),
+    "zf": sb([24], F32), "i896": sb([896], BF), "gt": sb([128], F32),
+    "idb": sb([128], BF), "nid": sb([128], BF), "idh": sb([128], F16), "nq": sb([128], F16),
+    "wm": sb([144], BF), "wh": sb([144], BF),
+    "bo": sb([128], BF), "nbo": sb([128], BF), "lt": sb([128], BF), "gm": sb([8], BF), "gm15": sb([8], BF),
+    "rw": sb([6, 8], BF), "dg": sb([6, 128], BF), "ids": sb([128], BF), "raw": sb([P], BF), "qi": sb([896], I32),
     "bq": sb([24], F32), "dl": sb([24], F32), "cd": sb([24], F32), "dj": sb([4], F32), "djr": sb([4], BF),
     "dja": sb([4], F32), "djb": sb([4], F32), "b2": sb([4], F32), "cc": sb([4], F32), "nw": sb([4], F32),
-    "ct": sb([24], F32), "pw": sb([336], BF), "cm": sb([8, 8, 16], BF), "cn": sb([8, 8, 16], BF),
-    "of1": sb([168], U16), "c2": sb([896], BF), "c3": sb([896], BF), "g2": sb([896], BF),
-    "tl": sb([112], U16), "xl": sb([112], U16),
+    "ct": sb([24], F32), "cm0": sb([8, 8, 16], BF), "cm1": sb([8, 8, 16], BF), "cm2": sb([8, 8, 16], BF),
+    "of1": sb([168], U16), "c0": sb([896], BF), "c1": sb([896], BF), "c2": sb([896], BF), "g2": sb([896], BF),
+    "tl": sb([112], F32), "xl": sb([112], F32), "cw": sb([168], BF),
     "ha0": sb([7, 3, 8], I32), "hb0": sb([7, 3, 8], I32), "ha1": sb([7, 3, 8], I32), "hb1": sb([7, 3, 8], I32),
     "ha2": sb([7, 3, 8], I32), "hb2": sb([7, 3, 8], I32),
     "off0": sb([168], U16), "off1": sb([168], U16), "off2": sb([168], U16), "off3": sb([256], U16),
-    "ja": sb([256], I32), "jb": sb([256], I32), "jh": sb([592], F16), "mk": sb([24, 424], BF),
+    "jh": sb([336], F16), "mk": sb([24, 256], BF), "th": sb([3, 24], I32), "xt": sb([4, 32], BF), "yt": sb([8], F32),
+    "tc": sb([256], BF), "ru": sb([128], BF), "rt": sb([128], BF), "w1": sb([144], BF),
 }
 for _b in ("pd0", "pd1", "pd2", "pd3", "pa", "pb", "px", "pq"):
     SCRATCH[_b] = ("psum", [128, 512], F32)
-SEMAPHORES = ["cv", "cs", "cp", "cg", "ldh", "ldc", "ldd", "ldr", "sty", "ls", "fl", "li0", "li1", "a0", "a1", "a2"]
+SEMAPHORES = ["cv", "cs", "cp", "cg", "ldh", "ldc", "ldd", "ldr", "sty", "ls", "fl", "li0", "li1", "li2", "a0", "a1", "a2",
+              "b0", "b1", "b2", "c0", "c1", "c2"]
 CNT = {"v": "cv", "s": "cs", "p": "cp", "g": "cg"}
 SYNC = 110.0
 
@@ -72,97 +90,94 @@ def engines_for(T, topo, a, b):
     return en
 
 
-def one_pass(ops, before, after, pr):
-    n = len(ops)
-    left = [len(before[i]) for i in range(n)]
-    rdy, free, fin, t0, order = {}, {}, [0.0] * n, [0.0] * n, []
-
-    def arrive(i):
-        t = 0.0
-        for d in before[i]:
-            same = (ops[d]["q"] == "p" and ops[i]["q"] == "p") or d not in ops[i]["deps"]
-            t = max(t, fin[d] + (-ops[d]["lat"] if same else SYNC if ops[i]["q"] else 0.0))
-        rdy[i] = t
-    for i in range(n):
-        if left[i] == 0:
-            arrive(i)
-    while rdy:
-        e = dict((i, max(rdy[i], free.get(ops[i]["q"], 0.0))) for i in rdy)
-        j = min(rdy, key=lambda i: (e[i], -pr[i], i))
-        q = ops[j]["q"]
-        if q:
-            now = [i for i in rdy if ops[i]["q"] == q and e[i] <= e[j] + 1.0]
-            j = max(now, key=lambda i: (pr[i], -i))
-            soon = [i for i in rdy if ops[i]["q"] == q and pr[i] > pr[j] + 600.0 and e[i] <= e[j] + 0.45 * ops[j]["cost"]]
-            if soon:
-                j = min(soon, key=lambda i: (e[i], i))
-            free[q] = e[j] + ops[j]["cost"]
-        t0[j] = e[j]
-        fin[j] = e[j] + ops[j]["cost"] + ops[j]["lat"]
-        order.append(j)
-        del rdy[j]
-        for k in after[j]:
-            left[k] -= 1
-            if left[k] == 0:
-                arrive(k)
-    return order, t0, fin
-
-
-def rank_of_part(t):
-    if t[:2] in ("ga", "ou", "oq") and t != "out":
-        return (4.0, 7.0, 9.0)[int(t[2])]
-    return {"sel0": 1.0, "cnt": 2.0, "sel1": 1.5, "sel2": 3.0, "hash1_0": 6.0, "tr1": 6.0, "hash2_0": 8.0, "tr2": 8.0,
-            "last": 8.5, "tr3": 8.5, "out": 10.0, "hash0_0": 0.5, "hash0_4": 0.6}.get(t, 0.0)
+def one_pass(ops, before, topological, free, pr):
+    pr = list(pr)
+    for i in topological:
+        for d, lag in before[i]:
+            if pr[i] >= pr[d]:
+                pr[i] = pr[d] - 1e-3
+    seq = sorted(topological, key=lambda i: -pr[i])
+    busy, end = dict((q, []) for q in "vspgyd"), [0.0] * len(ops)
+    for j in seq:
+        c, t = ops[j]["cost"], free[j]
+        for d, lag in before[j]:
+            if end[d] + lag > t:
+                t = end[d] + lag
+        if ops[j]["q"]:
+            b = busy[ops[j]["q"]]
+            k = len(b)
+            while k and b[k - 1][1] > t:
+                k -= 1
+            while k < len(b) and b[k][0] < t + c:
+                t = b[k][1]
+                k += 1
+            b.insert(k, (t, t + c))
+        end[j] = t + c
+    return seq, end
 
 
 def plan(ops):
     n = len(ops)
-    deps = [sorted(set(o["deps"] + o["ord"])) for o in ops]
-    kids = [[] for _ in range(n)]
-    for i in range(n):
-        for d in deps[i]:
-            kids[d].append(i)
-    pr = [0.0] * n
-    left, down = [len(k) for k in kids], []
-    todo = [i for i in range(n) if left[i] == 0]
-    while todo:
-        i = todo.pop()
-        down.append(i)
-        for d in deps[i]:
-            left[d] -= 1
-            if left[d] == 0:
-                todo.append(d)
-    for i in down:
-        pr[i] = ops[i]["cost"] + ops[i]["lat"] + max([pr[k] + SYNC for k in kids[i]] + [0.0])
+    deps, kids = [[] for _ in range(n)], [[] for _ in range(n)]
+    for i, o in enumerate(ops):
+        for d in sorted(set(o["deps"] + o["ord"])):
+            same = (ops[d]["q"] == "p" and o["q"] == "p") or d not in o["deps"]
+            lag = 0.0 if same else ops[d]["lat"] + (CFG["sync"] if o["q"] and o["q"] != "d" else 0.0)
+            deps[i].append((d, lag))
+            kids[d].append((i, lag))
+    zero, lat = [0.0] * n, [o["lat"] for o in ops]
     rs = np.random.RandomState(CFG["seed"])
+    up, down = list(range(n)), list(reversed(range(n)))
+    cases = []
+    for fc, fg, fl, fd in CFG["cases"]:
+        cost = [o["cost"] * (fd if o["q"] == "d" else fl if o["far"] else fg if "ind" in o else fc if o["q"] != "y" else 1.0)
+                for o in ops]
+        cases.append((cost, [[(d, lag * (fl if ops[d]["far"] else 1.0)) for d, lag in deps[i]] for i in range(n)]))
+
+    def replay(order, cost, before):
+        free, end = {}, [0.0] * n
+        for j in order:
+            t = free.get(ops[j]["q"], 0.0)
+            for d, lag in before[j]:
+                if end[d] + lag > t:
+                    t = end[d] + lag
+            end[j] = t + cost[j]
+            if ops[j]["q"]:
+                free[ops[j]["q"]] = end[j]
+        return max([end[i] + lat[i] for i in range(n)])
     tags = sorted(set([o["tag"] for o in ops]))
-    tix = [tags.index(o["tag"]) for o in ops]
-    best, off = None, [-1e5 * rank_of_part(t) for t in tags]
-    for it in range(CFG["tries"]):
-        new = list(off)
-        for _ in range(0 if it == 0 else 1 + it % 3):
-            new[int(rs.randint(len(tags)))] += float(rs.normal()) * (1e4, 5e4, 2e5)[it // 3 % 3]
-        up = [new[tix[i]] for i in range(n)]
-        for i in down:
-            for d in deps[i]:
-                up[d] = max(up[d], up[i])
-        order, t0, fin = one_pass(ops, deps, kids, [pr[i] + up[i] for i in range(n)])
-        if best is None or max(fin) <= best[0]:
-            best, off = (max(fin), order, t0), new
-    pr = [-t for t in best[2]]
-    for it in range(CFG["tries"]):
-        new = list(pr)
-        for _ in range(1 + it % 4):
-            k = int(rs.randint(n))
-            dv = float(rs.normal()) * 800.0
-            for i in range(k, min(n, k + 1 + it % 9)):
-                new[i] += dv
-        order, t0, fin = one_pass(ops, deps, kids, new)
-        if max(fin) <= best[0]:
-            best, pr = (max(fin), order, t0), new
+    back = [0.0] * n
+    for i in down:
+        due = [CFG["due"][w] for w in ops[i]["w"] if w in CFG["due"]]
+        back[i] = max([-CFG["due"]["end"] + lat[i]] + [-t for t in due] + [back[k] + ops[k]["cost"] + lag for k, lag in kids[i]])
+    back = [back[i] + ops[i]["cost"] for i in range(n)]
+    best = now = None
+    for it in range(CFG["tries"] + 1):
+        pr = list(back) if it % 2 == 0 or now is None else [-t for t in now[3]]
+        if it % 5 == 4:
+            tg, dv = tags[int(rs.randint(len(tags)))], float(rs.normal()) * 1500.0
+            pr = [pr[i] + (dv if ops[i]["tag"] == tg else 0.0) for i in range(n)]
+        else:
+            for _ in range(1 + it % 3 if it > 3 else 0):
+                k, dv = int(rs.randint(n)), float(rs.normal()) * 600.0
+                for i in range(k, min(n, k + 1 + it % 9)):
+                    pr[i] += dv
+        seq, end = one_pass(ops, deps, up, zero, pr)
+        t = max([end[i] + lat[i] for i in range(n)])
+        if now is not None and t > now[1] * 1.02:
+            continue
+        pos = dict((j, k) for k, j in enumerate(seq))
+        order = sorted(up, key=lambda i: (end[i] - ops[i]["cost"], pos[i]))
+        ts = [t] + [replay(order, cost, before) for cost, before in cases]
+        if now is None or sum(ts) <= now[0] + CFG["slack"] * (1.0 - it / CFG["tries"]):
+            now = (sum(ts), t, order, end, ts)
+            back = one_pass(ops, kids, down, lat, [end[i] + lat[i] for i in range(n)])[1]
+            if best is None or now[0] < best[0]:
+                best = now
     for i in range(n):
-        ops[i]["t0"] = best[2][i]
-    return best[1]
+        ops[i]["t0"] = best[3][i] - ops[i]["cost"]
+    CFG["est"] = best[4]
+    return best[2]
 
 
 def emit(g, T, ops, order, tail):
@@ -223,7 +238,7 @@ def emit(g, T, ops, order, tail):
 
 
 def build(T, topo, me):
-    ops, lastw, readers, tag = [], {}, {}, ["tab"]
+    ops, lastw, readers, tag, before = [], {}, {}, ["tab"], {}
 
     def add(q, fn, r=(), w=(), x=(), cost=0.0, lat=0.0, sem=None):
         deps = set()
@@ -236,7 +251,11 @@ def build(T, topo, me):
             deps.update([i for i in readers.get(k, []) if ops[i]["q"] != q])
         i = len(ops)
         ops.append({"q": q, "fn": fn, "deps": sorted(deps), "cost": cost, "lat": lat, "sem": sem, "w": list(w),
-                    "tag": tag[0], "ord": []})
+                    "tag": tag[0], "ord": [], "far": q == "g" and sem == "none"})
+        part = (tag[0][:3] if tag[0][:2] == "ou" else tag[0], q, w[0][:2] if tag[0][:2] == "ou" and q in ("v", "s") else "")
+        if q and tag[0] != "tab" and part in before:
+            ops[i]["ord"].append(before[part])
+        before[part] = i
         for k in list(r) + list(x):
             readers.setdefault(k, []).append(i)
         for k in w:
@@ -244,7 +263,7 @@ def build(T, topo, me):
             readers[k] = []
 
     def vc(n):
-        return 25.0 + 1.04 * max(64.0, n)
+        return CFG["fv"] + CFG["cy"] * max(64.0, n)
 
     def ts(out, a, s1, s2, o0, o1, n, r, w, x=()):
         if o1 is None:
@@ -265,24 +284,25 @@ def build(T, topo, me):
         add("v", lambda e: e.tensor_tensor_scan(out, a, b, init, o0, o1), r, w, x, vc(n))
 
     def act(out, a, n, r, w, x=(), fn=ACT.Identity, **kw):
-        add("s", lambda e: e.activation(out, a, fn, **kw), r, w, x, 65.0 + 1.04 * max(64.0, n))
+        add("s", lambda e: e.activation(out, a, fn, **kw), r, w, x, CFG["fs"] + CFG["cy"] * max(64.0, n))
 
     def mm(out, lt, rh, st, sp, n, r, bank):
-        add("p", lambda e: e.matmul(out, lt, rh, st, sp), r, [bank], (), 0.75 * max(64.0, n), 60.0)
+        add("p", lambda e: e.matmul(out, lt, rh, st, sp), r, [bank], (), CFG["pe"] * max(64.0, n), 60.0)
 
     def iota(out, pat, base, cm, n, w, flag=True):
         if flag:
-            add("g", lambda e: e.iota(out, pat, base, cm, allow_small_or_imprecise_dtypes=True), (), w, (), 150.0 + 2.1 * n)
+            add("g", lambda e: e.iota(out, pat, base, cm, allow_small_or_imprecise_dtypes=True), (), w, (), 150.0 + 1.7 * n)
         else:
-            add("g", lambda e: e.iota(out, pat, base, cm), (), w, (), 150.0 + 2.1 * n)
+            add("g", lambda e: e.iota(out, pat, base, cm), (), w, (), 150.0 + 1.7 * n)
 
     def gather(q, out, win, off, n, r, w, scale=None):
         if q == "s":
-            add("s", lambda e: e.activation(out, win.indirect(off), ACT.Identity, scale=scale or 1.0), r, w, (), 70.0 + 1.62 * n)
+            add("s", lambda e: e.activation(out, win.indirect(off), ACT.Identity, scale=scale or 1.0), r, w, (), CFG["fs"] + CFG["ga"] * n)
         elif scale:
-            add("v", lambda e: e.tensor_scalar(out, win.indirect(off), scale, None, ALU.mult), r, w, (), 55.0 + 1.62 * n)
+            add("v", lambda e: e.tensor_scalar(out, win.indirect(off), scale, None, ALU.mult), r, w, (), CFG["fv"] + CFG["ga"] * n)
         else:
-            add("v", lambda e: e.tensor_copy(out, win.indirect(off)), r, w, (), 55.0 + 1.62 * n)
+            add("v", lambda e: e.tensor_copy(out, win.indirect(off)), r, w, (), CFG["fv"] + CFG["ga"] * n)
+        ops[-1]["ind"] = True
 
     def dma(q, out, a, sem, r, w, lat=0.0):
         add(q, lambda e: e.dma_start(out, a).then_inc(T.sem[sem], 16), r, w, (), 60.0, lat, "none")
@@ -320,16 +340,17 @@ def build(T, topo, me):
             add("g", lambda e: e.remote_dma_fused(tr, local_sem=T.sem.ls), rd, [w + "i"], (), CFG["send"],
                 CFG["lat"], "none")
         far = len([l for l in ls if topo.chip(T.cores[order[l]]) != topo.chip(T.cores[me])])
-        t = 16 * max(far, 1) * (CFG["row"] + nb / 25.0)
+        t = 128 / min([bin(m).count("1") for o, a, ad, m in trs]) * (CFG["row"] + nb / 25.0)
         add("d" if far else None, None, [w + "i"], [w], (), t if far else 0.0, 0.0 if far else t, "none")
 
-    def exchange(out, a, sem, rd, w, lat):
-        for i, ls in enumerate(CFG["small"]):
-            send(ls, [out(l) for l in ls], [a(l) for l in ls], sem, rd, "x%s%d" % (sem, i), 32)
-        event(sem, got[sem], ["x%s%d" % (sem, i) for i in range(len(CFG["small"]))], w, lat)
+    def exchange(calls, out, a, sem, rd, w, nb, lat):
+        for i, ls in enumerate(calls):
+            send(ls, [out(l) for l in ls], [a(l) for l in ls], sem, rd, "x%s%d" % (sem, i), nb)
+        event(sem, got[sem], ["x%s%d" % (sem, i) for i in range(len(calls))], w, lat)
 
     col = lambda k: T.col[:, k:k + 1]
-    PC, GC, G16, W15, SN, M0, M4, MA, MB, H2 = range(10)
+    PC, GC, G16, W15, SN, M0, M4, MA, MB, H2, NA, NB, WR, Z0, Z1, G0, RC, S1 = range(18)
+    R0, R1 = range(2)
     hcs = lambda k: T.hcs[:, k:k + 1]
     seven = lambda s: [s % l for l in range(7)]
 
@@ -337,56 +358,74 @@ def build(T, topo, me):
     dma("s", T.cami[:, 112:336], T.came[:, 112:336], "ldd", (), ["l3"])
     dma("y", T.hcr[0:8, 0:21], T.hc[:], "ldh", ["l0"], ["l1"])
     dma("s", T.hcr[0:8, 21:22], T.had[:], "ldh", ["l3"], ["l2"])
-    dma("y", T.win[:, 0:P], T.ring[:], "ldr", ["l1"], ["l4"])
+    scaled = len(CFG["scale"]) > 0
+    dma("y", T.raw[:] if scaled else T.win[:, 0:P], T.ring[:], "ldr", ["l1"], ["l4"])
     event("ldh", 32, ["l1", "l2"], ["hcr"], 2100.0)
     event("ldc", 16, ["l0"], ["cami0"], 2100.0)
-    event("ldd", 16, ["l3"], ["cami1", "cami2"], 2300.0)
-    event("ldr", 16, ["l4"], ["rin"], 5500.0)
-    for i in range(4):
-        act(T.win[:, 1024 * i:1024 * i + 1024], T.win[:, 1024 * i:1024 * i + 1024], 1024, ["rin"], ["ring%d" % i],
-            scale=1.0 / 256)
+    event("ldd", 16, ["l3"], ["cami1"], 2300.0)
+    event("ldr", 16, ["l4"], ["ring"], 4500.0)
 
     iota(T.pi[:, 0:1], [[0, 1]], 0, 1, 1, ["pi"], False)
     iota(T.tg[:], [[1, 8], [0, 16]], 0, 0, 128, ["tg"])
     iota(T.ti[:], [[1, 144]], 0, 0, 144, ["ti"])
     iota(T.tabl[:], [[16, 7], [0, 8]], 0, 0, 56, ["tabl"])
-    iota(T.pt[:], [[16, 256]], 0, 1, 256, ["pt"])
+    iota(T.tc[:], [[16, 256]], 0, 0, 256, ["tc"])
+    iota(T.ru[:], [[0, 8], [1, 16]], 1, 0, 128, ["ru"])
+    ms(T.msk[:], 1.0, 112, ["msk"])
+    ms(T.msk[:, 0:224:16], 0.0, 14, ["msk"])
+    act(T.zf[:], T.msk[:, 0:24], 24, ["msk"], ["zf"], scale=0.0)
+    act(T.xt[:], T.msk[:, 0:128], 128, ["msk"], ["xt0"], scale=0.0)
+    act(T.so[:, 336:352], T.msk[:, 0:16], 16, ["msk"], ["soz"], scale=0.0)
+    act(T.bq[:, 22:24], T.msk[:, 0:2], 2, ["msk"], ["bq0"], scale=0.0, bias=-2048.0)
     for l, r in enumerate(order):
-        iota(T.tabr[:, :, 8 * l:8 * l + 8], [[128, 2], [0, 8]], TT * r, 0, 16, ["tabr%d" % l])
+        act(T.tab0[:, 8 * l:8 * l + 8], T.msk[:, 0:8], 8, ["msk"], ["tab0%d" % l], scale=0.0, bias=16.0 * (dfrom[l] - 1))
+        iota(T.tabr[:, 8 * l:8 * l + 8], [[0, 8]], TT * (r - l), 0, 8, ["tabr%d" % l])
     cp(col(PC), T.pi[:, 0:1], 1, ["pi"], ["pc"])
     ts(T.pi[:, 1:2], T.pi[:, 0:1], 4, None, ALU.arith_shift_right, None, 1, ["pi"], ["gi"])
     cp(col(GC), T.pi[:, 1:2], 1, ["gi"], ["gc"])
-    ts(col(G16), T.pi[:, 1:2], 16.0, None, ALU.mult, None, 1, ["gi"], ["g16"])
+    act(col(G16), col(GC), 1, ["gc"], ["g16"], scale=16.0)
     ts(col(W15), T.pi[:, 1:2], 16.0, 15.0, ALU.mult, ALU.add, 1, ["gi"], ["w15"])
     ts(col(SN), col(PC), col(W15), None, ALU.not_equal, None, 1, ["pc", "w15"], ["sn"])
     ts(T.gt[0:8, :], T.tg[0:8, :], T.col[0:8, PC:PC + 1], None, ALU.is_equal, None, 128, ["tg", "pc"], ["gt"])
     ts(T.idb[:], T.ti[:, 0:128], col(PC), None, ALU.is_equal, None, 64, ["ti", "pc"], ["idb"])
     ts(T.idh[:], T.ti[:, 0:128], col(PC), None, ALU.is_equal, None, 64, ["ti", "pc"], ["idh"])
+    hows = [how for m in CFG["mod"] for ls, how in m]
+    if "one" in hows:
+        act(T.ids[:], T.idb[:], 128, ["idb"], ["ids"], scale=1.0 / 256)
+    if "two" in hows:
+        ms(T.half[:, 0:128], -127.5, 64, ["half"])
+    if "s" in hows or "v" in hows:
+        ts(T.nq[:], T.ti[:, 0:128], col(PC), -256.0, ALU.is_equal, ALU.mult, 64, ["ti", "pc"], ["nq"])
     ts(T.wm[:], T.ti[:], col(W15), None, ALU.is_equal, None, 72, ["ti", "w15"], ["wm"])
     ts(T.bo[:], T.tg[:], col(GC), None, ALU.is_equal, None, 64, ["tg", "gc"], ["bo"])
-    ms(T.msk[:], 1.0, 56, ["msk"])
-    ms(T.msk[:, 0:112:16], 0.0, 7, ["msk"])
-    ms(T.zb[:], 0.0, 28, ["zb"])
-    ms(T.zf[:], 0.0, 24, ["zf"])
-    ts(T.gm[:], T.ti[:, 0:8], col(GC), None, ALU.is_equal, None, 8, ["ti", "gc"], ["gm"])
-    ts(T.r1[:], T.ti[:, 0:8], col(GC), col(SN), ALU.is_equal, ALU.mult, 8, ["ti", "gc", "sn"], ["r1"])
-    act(T.r16[:], T.r1[:], 8, ["r1"], ["r16"], scale=16.0)
-    act(T.r8[:], T.r1[:], 8, ["r1"], ["r8"], scale=8.0)
-    act(T.rh[:], T.r1[:], 8, ["r1"], ["rh"], scale=0.5)
+    ts(T.rw[:, R0, 0:7], T.tab0[:, 0:56:8], col(G16), col(SN), ALU.is_equal, ALU.mult, 8, seven("tab0%d") + ["g16", "sn"], ["r0"])
+    act(T.rw[:, R1, :], T.bo[:, 0:128:16], 8, ["bo", "sn"], ["r1"], scale=col(SN))
+    for k in set([(R0, R0, R1)[z] for z in range(3) if CFG["sel"][z][0] == "s"]):
+        act(T.rw[:, k + 2, 0:7], T.rw[:, k, 0:7], 8, ["r%d" % k], ["r%d" % (k + 2)], scale=0.5)
+    act(T.tabx[:], T.tab0[:], 56, seven("tab0%d"), ["tabx"], scale=-16.0, bias=float(TT * me))
     act(T.wh[:], T.wm[:], 144, ["wm"], ["wh"], scale=0.5)
+    act(col(S1), col(SN), 1, ["sn"], ["s1"], scale=-1.0, bias=1.0)
+    act(T.w1[:], T.wm[:], 144, ["wm", "s1"], ["w1"], scale=col(S1))
+    act(col(RC), col(G16), 1, ["g16", "pc"], ["rc"], scale=-1.0, bias=col(PC))
+    add("g", lambda e: e.affine_select(T.rt[:], T.ru[:], [[-16, 8], [0, 16]], ALU.is_ge, 0.0, 0, 1), ["ru"], ["rt0"], (), 400.0)
+    add("g", lambda e: e.affine_select(T.rt[:], T.rt[:], [[16, 8], [0, 16]], ALU.is_ge, 0.0, 15, -1), ["rt0"], ["rt"], (), 400.0)
     act(T.nid[:], T.idb[:], 128, ["idb"], ["nid"], scale=-1.0)
     act(T.nbo[:], T.bo[:], 128, ["bo"], ["nbo"], scale=-1.0)
     add("g", lambda e: e.affine_select(T.lt[:], T.nbo[:], [[-1, 128]], ALU.is_gt, 0.0, 0, 1), ["nbo"], ["lt"], (), 450.0)
-    for l in range(7):
-        act(T.i896[:, 128 * l:128 * l + 128], T.ti[:, 0:128], 128, ["ti"], ["i896_%d" % l])
+    iota(T.i896[:, 0:512], [[0, 4], [1, 128]], 0, 0, 512, ["i896_0"])
+    act(T.i896[:, 512:896], T.i896[:, 0:384], 384, ["i896_0"], ["i896_1"])
+    I896 = ["i896_0", "i896_1"]
 
     tag[0] = "hc"
-    cp(T.hcf[0:8, 0:22], T.hcr[0:8, 0:22], 22, ["hcr"], ["hcf"])
-    mm(T.pq[:, 0:22], T.gt[0:8, :], T.hcf[0:8, 0:22], True, True, 256, ["gt", "hcf"], "pq")
-    cp(T.hcs[:, 0:22], T.pq[:, 0:22], 22, (), ["hcs"], ["pq"])
+    ts(T.hcr[0:8, 22:23], T.hcr[0:8, 21:22], P - 1, None, ALU.bitwise_and, None, 1, ["hcr"], ["hcm"])
+    cp(T.hcf[0:8, 0:23], T.hcr[0:8, 0:23], 23, ["hcr", "hcm"], ["hcf"])
+    mm(T.pq[:, 0:23], T.gt[0:8, :], T.hcf[0:8, 0:23], True, True, 256, ["gt", "hcf"], "pq")
+    act(T.hcs[:, 0:23], T.pq[:, 0:23], 23, (), ["hcs"], ["pq"])
     ts(T.cc[:, 0:1], hcs(21), float(P), 1.0 / P, ALU.min, ALU.mult, 1, ["hcs"], ["cc0"])
     for k in range(3):
         act(T.dg[:, k, :], T.idb[:], 128, ["idb", "hcs"], ["dg%d" % k], scale=hcs(18 + k))
+        if "one" in hows:
+            act(T.dg[:, 3 + k, :], T.ids[:], 128, ["ids", "hcs"], ["dg%d" % (3 + k)], scale=hcs(18 + k))
 
     def hashes(e, l0, l1, xs, xr, xx, bank):
         tag[0] = "hash%d_%d" % (e, l0)
@@ -411,7 +450,7 @@ def build(T, topo, me):
 
     def translate(e, j, kj, n, bank):
         L, tag[0] = 7 * e, "tr%d" % e
-        s0, m0 = 168 * (e - 1), 168 * (e // 3)
+        s0, m0 = 168 * (e - 1), 0
         jh, acc, kh = T.jh[:, s0:s0 + n], T[bank][:, 0:n], "jh%d" % e
         ts(jh, j, 2048.0, None, ALU.subtract, None, n, [kj], [kh])
         mm(acc, T.idh[:], jh, True, False, n, ["idh", kh], bank)
@@ -423,139 +462,221 @@ def build(T, topo, me):
             mm(acc, T.idb[:], T.mk[:, i, m0:m0 + n], False, i == len(steps) - 1, n, ["idb", km], bank)
         ts(T["off%d" % e][:], acc, float(P + 2048), None, ALU.add, None, n, (), ["off%d" % e], [bank])
 
-    def rows(out, win, off, b, r, w):
-        add("v", lambda e: e.tensor_tensor(out, win.indirect(off), b, ALU.is_le), r, w, (), 55.0 + 1.62 * 448)
-
-    def select(z, sv, fv, ks, kf, ba, bb, bx):
-        u, tag[0] = CFG["sel"][z], "sel%d" % z
-        v = u == "v"
-        cm, c2, A, B, X = (T.cm if v else T.cn), (T.c2 if v else T.c3), T[ba], T[bb], T[bx]
-        ct, pw, of1 = T.ct[0:112, 8 * z:8 * z + 8], T.pw[:, 112 * z:112 * z + 112], T.of1[:, 56 * z:56 * z + 56]
-        mm(B[:, 0:112], T.bo[:], sv, True, False, 112, ["bo"] + ks, bb)
-        mm(B[:, 0:112], T.lt[:], fv, False, True, 112, ["lt"] + kf, bb)
-        act(pw, B[:, 0:112], 112, (), ["pw%d" % z], [bb])
-        mm(A[0:112, 112:120], sv, T.gm[:], True, True, 8, ["gm"] + ks, ba)
-        if not v:
-            act(ct, A[0:112, 112:120], 8, (), ["ct%d" % z], [ba], scale=-1.0, bias=0.5)
-        kc = [u + "cm_%d" % a for a in range(8)]
+    def select(z, tot, ktot, gm, pw, kpw, tab, ba, bd, parts):
+        (u1, u2), tag[0] = CFG["sel"][z], "sel%d" % z
+        cm, c2, A = T["cm%d" % z], T["c%d" % z], T[ba]
+        ra = (R0 if z < 2 else R1) + (0 if u1 == "v" else 2)
+        kr = ["r%d" % ra]
+        mm(A[0:112, 112:120], tot, gm, True, True, 8, ["bo", "idb"] + ktot, ba)
+        if u1 == "s":
+            act(T.ct[0:112, 8 * z:8 * z + 8], A[0:112, 112:120], 8, (), ["ct%d" % z], [ba], scale=-1.0, bias=0.5)
+        kc = ["cm%d_%d" % (z, a) for a in range(8)]
         for a in range(8):
-            if v:
+            if u1 == "v":
                 ts(cm[0:112, :, a, :], T.ti[0:112, 0:128], A[0:112, 112 + a:113 + a], None, ALU.is_ge, None, 64, ["ti"],
                    [kc[a]], [ba])
             else:
                 act(cm[0:112, :, a, :], T.ti[0:112, 0:128], 128, ["ti", "ct%d" % z], [kc[a]], fn=ACT.Sign,
                     bias=T.ct[0:112, 8 * z + a:8 * z + a + 1])
-        mm(A[:, 128:184], T.idb[:], T.tabl[:], True, False, 56, ["idb", "tabl"], ba)
+        mm(A[:, 128:184], T.idb[:], tab[:], True, False, 56, ["idb", "tabl"] + seven("tab0%d"), ba)
         for a in range(8):
-            mm(A[:, 128 + a:184:8], cm[0:112, a], (T.r1 if v else T.rh)[0:112, 0:7], False, a == 7, 7, kc + ["r1", "rh"], ba)
-        ts(of1, A[:, 128:184], 0.0 if v else 7.5, None, ALU.add, None, 56, (), ["of1%d" % z], [ba])
-        if z < 2:
-            mm(X[:, 0:56], T.idb[:], T.zb[:], True, False, 56, ["idb", "zb"], bx)
-        else:
-            mm(X[:, 0:56], T.idb[:], T.tabr[:, 0 if v else 1, :], True, False, 56, ["idb"] + seven("tabr%d"), bx)
-        for a in range(8):
-            mm(X[:, a:56:8], cm[0:112, a], (T.r16 if v else T.r8)[0:112, 0:7], False, False, 7, kc + ["r16", "r8"], bx)
-        bd = (bb, ba)
-        for h in range(2):
-            c0, D, oh = 448 * h, T[bd[h]][:, 0:448], T.of1[:, 56 * z + 28 * h:56 * z + 28 * h + 28]
-            if v:
-                rows(c2[:, c0:c0 + 448], pw, oh, T.i896[:, c0:c0 + 448], ["pw%d" % z, "of1%d" % z] + seven("i896_%d"),
-                     ["vc2_%d" % h])
+            mm(A[:, 128 + a:184:8], cm[0:112, a], T.rw[0:112, ra, 0:7], False, a == 7, 7, kc + kr, ba)
+        ts(T.of1[:, 56 * z:56 * z + 56], A[:, 128:184], 0.0 if u1 == "v" else 7.5, None, ALU.add, None, 56, (),
+           ["of1%d" % z], [ba])
+        act(T.cw[:, 56 * z:56 * z + 56], A[:, 128:184], 56, (), ["cw%d" % z], [ba], scale=16.0,
+            bias=120.0 * (u1 == "s") + 8.0 * (u2 == "s"))
+        for l0, l1, bx in parts:
+            tag[0] = "sel%d" % z + ("" if z else "b" if l0 else "a")
+            mm(T[bx][:, 0:8 * (l1 - l0)], T.idb[:], (T.tabr if z == 2 else T.tabx)[:, 8 * l0:8 * l1], True, False, 56,
+               ["idb"] + (seven("tabr%d") if z == 2 else ["tabx"]), bx)
+            mm(T[bx][:, 0:8 * (l1 - l0)], T.idb[:], T.cw[:, 56 * z + 8 * l0:56 * z + 8 * l1], False, False, 56,
+               ["idb", "cw%d" % z], bx)
+        for h, (l0, l1) in enumerate(((0, 4), (4, 7))):
+            c0, c1, oh = CAP * l0, CAP * l1, T.of1[:, 56 * z + 8 * l0:56 * z + 8 * l1]
+            kh, tag[0] = "c%d_%d" % (z, h), "sel%d" % z + ("" if z else "ab"[h])
+            if u2 == "v":
+                add("v", lambda e, c0=c0, c1=c1, oh=oh: e.tensor_tensor(c2[:, c0:c1], pw.indirect(oh), T.i896[:, c0:c1], ALU.is_le),
+                    kpw + ["of1%d" % z] + I896, [kh], (), CFG["fv"] + CFG["ga"] * (c1 - c0))
+                ops[-1]["ind"] = True
             else:
-                gather("s", T.g2[:, c0:c0 + 448], pw, oh, 448, ["pw%d" % z, "of1%d" % z], ["g2_%d" % h])
-                mm(D, T.idb[:], T.i896[:, c0:c0 + 448], True, False, 448, ["idb"] + seven("i896_%d"), bd[h])
-                mm(D, T.nid[:], T.g2[:, c0:c0 + 448], False, True, 448, ["nid", "g2_%d" % h], bd[h])
-                act(c2[:, c0:c0 + 448], D, 448, (), ["sc2_%d" % h], [bd[h]], fn=ACT.Sign, bias=0.5)
-        for s in range(16):
-            mm(X[:, 0:56], (T.wm if v else T.wh)[:, 15 - s:143 - s], c2[:, s:896:16], False, s == 15, 56,
-               ["wm", "wh", u + "c2_0", u + "c2_1"], bx)
-        if z < 2:
-            c = 56 * z
-            ts(T.tl[:, c:c + 56], X[:, 0:56], TT * me + (0.0 if v else 128.0), None, ALU.add, None, 56, (), ["tl%d" % z], [bx])
-            exchange(lambda l: T.xl[:, c + 8 * back[l]:c + 8 * back[l] + 8],
-                     lambda l: T.tl[:, c + 8 * dfrom[l] - 8:c + 8 * dfrom[l]], "li%d" % z, ["tl%d" % z], ["xl%d" % z], 200.0)
+                D = T[bd[h]][:, 0:c1 - c0]
+                gather("s", T.g2[:, c0:c1], pw, oh, c1 - c0, kpw + ["of1%d" % z], ["g2_%d" % h])
+                mm(D, T.idb[:], T.i896[:, c0:c1], True, False, c1 - c0, ["idb"] + I896, bd[h])
+                mm(D, T.nid[:], T.g2[:, c0:c1], False, True, c1 - c0, ["nid", "g2_%d" % h], bd[h])
+        for h, (l0, l1) in enumerate(((0, 4), (4, 7))):
+            c0, c1 = CAP * l0, CAP * l1
+            if u2 == "s":
+                act(c2[:, c0:c1], T[bd[h]][:, 0:c1 - c0], c1 - c0, (), ["c%d_%d" % (z, h)], [bd[h]], fn=ACT.Sign, bias=0.5)
+        for l0, l1, bx in parts:
+            tag[0] = "sel%d" % z + ("" if z else "b" if l0 else "a")
+            for s in range(16):
+                mm(T[bx][:, 0:8 * (l1 - l0)], (T.wm if u2 == "v" else T.wh)[:, 15 - s:143 - s], c2[:, CAP * l0 + s:CAP * l1:16],
+                   False, s == 15, 56, ["wm", "wh"] + ["c%d_%d" % (z, h) for h in range(2) if l0 < (4, 7)[h] and l1 > (0, 4)[h]], bx)
 
     def packets(e, wkeys):
-        n, first = CAP, len(ops)
+        n = CAP
         ga, ou, off = T["ga%d" % e], T["ou%d" % e], T["off%d" % e]
-        win = T.win[:, 0:P + 896 * e]
-        for l in range(7):
-            nv, tag[0] = CFG["nv"][e][l], "ga%d_%d" % (e, l)
-            for q, k0, k1 in (("v", 0, nv), ("s", nv, 3)):
-                if k1 > k0:
-                    gather(q, ga[:, (3 * l + k0) * n:(3 * l + k1) * n], win, off[:, (3 * l + k0) * 8:(3 * l + k1) * 8],
-                           (k1 - k0) * n, wkeys + ["off0_%d" % l if e == 0 else "off%d" % e],
-                           ["ga%d_%d_%d" % (e, l, k) for k in range(k0, k1)])
-            bank, tag[0] = "pd%d" % (l % 4), "oq%d_%d" % (e, l)
-            ps = T[bank][:, 0:n]
-            for k in range(3):
-                mm(ps, T.dg[:, k, :], ga[:, (3 * l + k) * n:(3 * l + k + 1) * n], k == 0, k == 2, n,
-                   ["dg%d" % k, "ga%d_%d_%d" % (e, l, k)], bank)
-            qq = T.qq[:, l * n:l * n + n]
-            ts(qq, ps, 127.5 / 256, None, ALU.subtract, None, n, (), ["qq%d" % l], [bank])
-            tag[0] = "ou%d_%d" % (e, l)
-            tt(ou[:, l * n:(l + 1) * n], ps, qq, ALU.subtract, n, ["qq%d" % l], ["ou%d_%d" % (e, l)], [bank])
-        for i, ls in enumerate(CFG["calls"]):
-            tag[0] = "ou%d_%d" % (e, max(ls))
-            send(ls, [T.win[:, P + 896 * e + (dto[l] - 1) * n:P + 896 * e + dto[l] * n] for l in ls],
-                 [ou[:, l * n:(l + 1) * n] for l in ls], "a%d" % e, ["ou%d_%d" % (e, l) for l in ls], "s%d_%d" % (e, i), 2 * n)
-        for q in "vs":
-            mine, last = [i for i in range(first, len(ops)) if ops[i]["q"] == q], None
-            for w in CFG["c" + q].split():
-                for i in [i for i in mine if ops[i]["tag"] == "%s%d_%s" % ({"g": "ga", "q": "oq", "o": "ou"}[w[0]], e, w[1])]:
-                    if last is not None:
-                        ops[i]["ord"].append(last)
-                    last = i
-        event("a%d" % e, got["a%d" % e], ["s%d_%d" % (e, i) for i in range(len(CFG["calls"]))], ["log%d" % e], 200.0)
+        win = T.raw[:] if scaled and e == 0 else T.win[:, 0:P + 896 * e]
+        last, banks = {}, [0]
+        u0 = 0
+        for run in CFG["pick"][e].split():
+            q, u1 = run[0], u0 + len(run)
+            tag[0] = "ga%d_%d" % (e, u0 // 3)
+            gather(q, ga[:, u0 * n:u1 * n], win, off[:, u0 * 8:u1 * 8], (u1 - u0) * n,
+                   wkeys + (["off0_%d" % (u // 3) for u in range(u0, u1)] if e == 0 else ["off%d" % e]),
+                   ["ga%d_%d" % (e, u) for u in range(u0, u1)])
+            if q in last:
+                ops[-1]["ord"].append(last[q])
+            last[q], u0 = len(ops) - 1, u1
 
+        def weighted(ls, first, stop=True, low=False):
+            bank = "pd%d" % (banks[0] % 4)
+            banks[0] += 1
+            ps = T[bank][:, 0:n * len(ls)]
+            for i, l in enumerate(ls):
+                part = T[bank][:, n * i:n * i + n]
+                if first is not None:
+                    mm(part, T.idb[:], first, True, False, n, ["idb", "half"], bank)
+                for k in range(3):
+                    kd, u = k + (3 if low else 0), 3 * l + k
+                    mm(part, T.dg[:, kd, :], ga[:, n * u:n * u + n], k == 0 and first is None, k == 2 and stop, n,
+                       ["dg%d" % kd, "ga%d_%d" % (e, u)], bank)
+                if not stop:
+                    mm(part, T.nq[:], T.qh[:, n * l:n * l + n], False, True, n, ["nq", "qq%d" % l], bank)
+            return bank, ps
+        for ls, how in CFG["mod"][e]:
+            tag[0] = "ou%d_%d" % (e, ls[0])
+            c0, c1, w = n * ls[0], n * ls[-1] + n, n * len(ls)
+            ko, kq = ["ou%d_%d" % (e, l) for l in ls], ["qq%d" % l for l in ls]
+            if how == "one":
+                bank, ps = weighted(ls, None, True, e == 0 or not scaled)
+                ts(T.qi[:, c0:c1], ps, 127.5 / 256, None, ALU.subtract, None, w, (), kq, [bank])
+                tt(ou[:, c0:c1], ps, T.qi[:, c0:c1], ALU.subtract, w, kq, ko, [bank])
+            elif how == "two":
+                bank, ps = weighted(ls, T.half[:, 0:n])
+                bank2, ps2 = weighted(ls, None)
+                ts(T.qf[:, c0:c1], ps, MAGIC, MAGIC, ALU.add, ALU.subtract, w, (), kq, [bank])
+                tt(ou[:, c0:c1], ps2, T.qf[:, c0:c1], ALU.subtract, w, kq, ko, [bank2])
+            else:
+                bank, ps = weighted(ls, None)
+                ts(T.qh[:, c0:c1], ps, 1.0 / 256, QOFF - 127.5 / 256, ALU.mult, ALU.add, w, (), kq, [bank])
+                bank, ps = weighted(ls, None, False)
+                if how == "s":
+                    act(ou[:, c0:c1], ps, w, (), ko, [bank], bias=256.0 * QOFF)
+                else:
+                    ts(ou[:, c0:c1], ps, 256.0 * QOFF, None, ALU.add, None, w, (), ko, [bank])
+        small = [l for ls, how in CFG["mod"][e] for l in ls if how == "one" and not scaled]
+        for i, ls in enumerate(CFG["lots"]):
+            sem = "%s%d" % ("abc"[i], e)
+            for l in ls:
+                tag[0] = "ou%d_%d" % (e, l)
+                send([l], [T.win[:, P + 896 * e + (dto[l] - 1) * n:P + 896 * e + dto[l] * n]], [ou[:, l * n:(l + 1) * n]],
+                     sem, ["ou%d_%d" % (e, l)], "s%d_%d" % (e, l), 2 * n)
+            event(sem, got[sem], ["s%d_%d" % (e, l) for l in ls], ["log%d_%d" % (e, l) for l in ls], 200.0)
+            for l in ls:
+                if l in small:
+                    seg = T.win[:, P + 896 * e + (dfrom[l] - 1) * n:P + 896 * e + dfrom[l] * n]
+                    if CFG["up"][e][l] == "s":
+                        act(seg, seg, n, (), ["log%d_%d" % (e, l)], scale=256.0)
+                    else:
+                        ts(seg, seg, 256.0, None, ALU.mult, None, n / 2, (), ["log%d_%d" % (e, l)])
+
+    for z, c0, c1, bank in ((0, 0, 112, "pb"), (1, 112, 336, "pd2")):
+        tag[0], w = ("sel0", "flags")[z], c1 - c0
+        cp(T.fo[:, c0:c1], T.cami[:, c0:c1], w, ["cami%d" % z], ["fo%d" % z])
+        scan(T.so[:, c0:c1], T.msk[:, 0:w], T.fo[:, c0:c1], 0.0, ALU.mult, ALU.add, w / 2, ["fo%d" % z, "msk"], ["so%d" % z])
+        mm(T[bank][:, 0:w], T.bo[:], T.so[:, c0:c1], True, False, w, ["bo", "so%d" % z], bank)
+        mm(T[bank][:, 0:w], T.lt[:], T.fo[:, c0:c1], False, True, w, ["lt", "fo%d" % z], bank)
+    tag[0] = "sel0"
+    act(T.pw0[:], T.pb[:, 0:112], 112, (), ["pw0"], ["pb"])
     tag[0] = "flags"
-    for e in range(3):
-        c = slice(112 * e, 112 * e + 112)
-        cp(T.fo[:, c], T.cami[:, c], 112, ["cami%d" % e], ["fo%d" % e])
-        scan(T.so[:, c], T.msk[:], T.fo[:, c], 0.0, ALU.mult, ALU.add, 56, ["fo%d" % e, "msk"], ["so%d" % e])
-    exchange(lambda l: T.fr[:, 16 * back[l]:16 * back[l] + 16], lambda l: T.fo[:, 208 + 16 * dfrom[l]:224 + 16 * dfrom[l]],
-             "fl", ["fo2"], ["fr"], CFG["first"])
-    select(0, T.so[:, 0:112], T.fo[:, 0:112], ["so0"], ["fo0"], "pa", "pb", "px")
-    select(1, T.so[:, 112:224], T.fo[:, 112:224], ["so1"], ["fo1"], "pd2", "pd2", "pd3")
+    act(T.pwo[:], T.pd2[:, 0:224], 224, (), ["pwo"], ["pd2"])
+    exchange(CFG["small"], lambda l: T.pwr[:, 16 * back[l]:16 * back[l] + 16],
+             lambda l: T.pwo[:, 96 + 16 * dfrom[l]:112 + 16 * dfrom[l]], "fl", ["pwo"], ["pwr"], 32, CFG["first"])
+
+    def lists(h, z, l0, l1, bx, calls):
+        c = 56 * z
+        (cp if CFG["tl"][h] == "v" else act)(T.tl[:, c + 8 * l0:c + 8 * l1], T[bx][:, 0:8 * (l1 - l0)], 56, (), ["tl%d" % h], [bx])
+        exchange(calls, lambda l: T.xl[:, c + 8 * back[l]:c + 8 * back[l] + 8], lambda l: T.tl[:, c + 8 * l:c + 8 * l + 8],
+                 "li%d" % h, ["tl%d" % h], ["xl%d" % h], 32, 200.0)
+    halves = CFG["halves"]
+    select(0, T.so[:, 0:112], ["so0"], T.bo[:, 0:128:16], T.pw0[:], ["pw0"], T.tab0, "pa", None, halves)
+    for h, (l0, l1, bx) in enumerate(halves):
+        tag[0] = "sel0" + "ab"[h]
+        lists(h, 0, l0, l1, bx, CFG["lists"][h])
+    select(1, T.so[:, 112:224], ["so1"], T.bo[:, 0:128:16], T.pwo[:, 0:112], ["pwo"], T.tab0, "pd1", ("pd2", "pa"), ((0, 7, "pb"),))
+    lists(2, 1, 0, 7, "pb", CFG["small"])
     tag[0] = "cnt"
-    mm(T.pq[:, 32:53], T.bo[:], T.so[:, 15:336:16], True, True, 21, ["bo", "so0", "so1", "so2"], "pq")
-    scan(T.bq[:, 0:21], T.pq[:, 32:53], T.zf[:, 0:21], -2048.0, ALU.add, ALU.add, 21, ["zf"], ["bq"], ["pq"])
-    ts(T.dl[:, 0:21], T.pq[:, 32:53], -1.0, float(CAP), ALU.mult, ALU.add, 21, (), ["dl"], ["pq"])
+    mm(T.pq[:, 32:54], T.bo[:], T.so[:, 15:352:16], True, True, 22, ["bo", "so0", "so1", "soz"], "pq")
+    scan(T.bq[:, 0:22], T.pq[:, 32:54], T.zf[:, 0:22], -2048.0, ALU.add, ALU.add, 22, ["zf"], ["bq"], ["pq"])
+    act(T.dl[:, 0:21], T.pq[:, 32:53], 21, (), ["dl"], ["pq"], scale=-1.0, bias=float(CAP))
     scan(T.cd[:, 0:21], T.dl[:, 0:21], T.zf[:, 0:21], 0.0, ALU.add, ALU.add, 21, ["zf", "dl"], ["cd"])
-    cp(T.pi[:, 2:3], hcs(21), 1, ["hcs"], ["mi"])
-    ts(T.pi[:, 3:4], T.pi[:, 2:3], P - 1, None, ALU.bitwise_and, None, 1, ["mi"], ["mj"])
-    ts(col(M4), T.pi[:, 3:4], float(P), None, ALU.mult, None, 1, ["mj"], ["m4"])
-    ts(col(MA), T.pi[:, 3:4], float(P), None, ALU.subtract, None, 1, ["mj"], ["ma"])
-    ts(col(MB), T.pi[:, 3:4], -1.0, 2048.0, ALU.mult, ALU.add, 1, ["mj"], ["mb"])
-    ts(col(M0), T.pi[:, 3:4], col(G16), None, ALU.add, None, 1, ["mj", "g16"], ["m0"])
-    ts(col(H2), hcs(21), 2048.0, None, ALU.add, None, 1, ["hcs"], ["h2"])
-    ts(T.dj[:, 0:3], T.cd[:, 5:21:7], -1.0, col(MA), ALU.mult, ALU.add, 3, ["cd", "ma"], ["dj"])
-    cp(T.djr[:, 0:3], T.dj[:, 0:3], 3, ["dj"], ["djr"])
-    cp(T.dja[:, 0:3], T.djr[:, 0:3], 3, ["djr"], ["dja"])
+    act(col(M4), hcs(22), 1, ["hcs"], ["m4"], scale=float(P))
+    act(col(MA), hcs(22), 1, ["hcs"], ["ma"], bias=-float(P))
+    act(col(MB), hcs(22), 1, ["hcs"], ["mb"], scale=-1.0, bias=2048.0)
+    act(col(M0), hcs(22), 1, ["hcs"], ["m0"], bias=2048.0)
+    act(col(NA), hcs(22), 1, ["hcs"], ["na"], scale=-1.0, bias=float(P))
+    act(col(NB), hcs(22), 1, ["hcs"], ["nb"], scale=-1.0, bias=2.0 * P)
+    act(col(H2), hcs(21), 1, ["hcs"], ["h2"], bias=2048.0)
+    act(T.dj[:, 0:3], T.cd[:, 5:21:7], 3, ["cd", "ma"], ["dj"], scale=-1.0, bias=col(MA))
+    act(T.djr[:, 0:3], T.dj[:, 0:3], 3, ["dj"], ["djr"])
+    act(T.dja[:, 0:3], T.djr[:, 0:3], 3, ["djr"], ["dja"])
     tt(T.djb[:, 0:3], T.dj[:, 0:3], T.djr[:, 0:3], ALU.subtract, 6, ["dj", "djr"], ["djb"])
     ts(T.b2[:, 0:3], T.bq[:, 6:21:7], col(MB), None, ALU.max, None, 3, ["bq", "mb"], ["b2"])
     ts(T.cc[:, 1:3], T.bq[:, 6:14:7], col(H2), float(P), ALU.add, ALU.min, 2, ["bq", "h2"], ["cc12"])
-    ts(T.nw[:, 0:1], T.bq[:, 20:21], col(H2), None, ALU.add, None, 1, ["bq", "h2"], ["nw"])
+    act(T.nw[:, 0:1], T.bq[:, 20:21], 1, ["bq", "h2"], ["nw"], bias=col(H2))
     dma("y", T.now[:], T.nw[0:128:16, 0:1], "sty", ["nw"], ["now"], 2000.0)
 
-    tag[0] = "sel2"
-    scan(T.sr[:], T.msk[:], T.fr[:], 0.0, ALU.mult, ALU.add, 56, ["fr", "msk"], ["sr"])
-    select(2, T.sr[:], T.fr[:], ["sr"], ["fr"], "pb", "pb", "pq")
-    hashes(0, 0, 4, T.xl[:, 0:32], ["xl0"], [], "pd0")
-    hashes(0, 4, 7, T.xl[:, 32:56], ["xl0"], [], "pd1")
-    hashes(1, 0, 7, T.xl[:, 56:112], ["xl1"], [], "pa")
-    hashes(2, 0, 7, T.pq[:, 0:56], [], ["pq"], "px")
+    for h, (l0, l1) in enumerate(CFG["hash0"]):
+        hashes(0, l0, l1, T.xl[:, 8 * l0:8 * l1], ["xl%d" % i for i, x in enumerate(halves) if x[0] < l1 and x[1] > l0], [], "pd%d" % h)
+    hashes(1, 0, 7, T.xl[:, 56:112], ["xl2"], [], "pa")
+    select(2, T.pwr[:], ["pwr"], T.idb[:, 15:128:16], T.pwr[:], ["pwr"], T.tabl, "px", ("px", "pb"), ((0, 7, "pq"),))
+    hashes(2, 0, 7, T.pq[:, 0:56], [], ["pq"], "pb")
     tag[0] = "last"
-    ts(T.ja[:], T.pt[:], col(M0), None, ALU.subtract, None, 256, ["pt", "m0", "tl0"], ["ja"])
-    ts(T.jb[:], T.ja[:], P - 1, None, ALU.bitwise_and, None, 256, ["ja"], ["jb"])
-    translate(3, T.jb[:], "jb", 256, "pb")
-    logs = ["ring0", "ring1", "ring2", "ring3", "log0", "log1", "log2"]
+    xq = lambda q, a, b: T.xt[:, q, a:b]
+    ts(T.th[:, 2, :], T.bq[:, 0:24], col(M0), None, ALU.add, None, 24, ["bq", "bq0", "m0"], ["th"])
+    ts(T.th[:, 0, :], T.th[:, 2, :], P - 16, None, ALU.bitwise_and, None, 24, ["th"], ["thh"])
+    ts(T.th[:, 1, :], T.th[:, 2, :], 15, None, ALU.bitwise_and, None, 24, ["th"], ["thl"])
+    cp(T.xt[:, 0:2, 0:24], T.th[:, 0:2, :], 48, ["thh", "thl", "xt0"], ["xt1"])
+    ts(col(WR), T.th[:, 2, 20:21], float(P), None, ALU.is_ge, None, 1, ["th"], ["wr"])
+    ts(xq(3, 0, 20), T.th[:, 2, 0:20], float(P), col(WR), ALU.is_lt, ALU.mult, 20, ["th", "wr", "xt0"], ["xt2"])
+    act(xq(2, 0, 20), T.dl[:, 0:20], 20, ["dl", "xt0"], ["xt3"])
+    act(col(Z0), col(WR), 1, ["wr", "ma"], ["z0"], scale=-float(P), bias=col(MA))
+    act(col(Z1), T.cd[:, 19:20], 1, ["cd", "z0"], ["z1"], scale=-1.0, bias=col(Z0))
+    act(xq(2, 20, 21), col(Z1), 1, ["z1", "xt0"], ["xt4"])
+    act(xq(2, 21, 22), xq(2, 20, 21), 1, ["z1", "xt4"], ["xt5"], scale=-1.0, bias=col(Z1))
+    act(xq(2, 22, 23), col(NA), 1, ["na", "xt0"], ["xt6"])
+    act(xq(2, 23, 24), xq(2, 22, 23), 1, ["na", "xt6"], ["xt7"], scale=-1.0, bias=col(NA))
+    act(col(G0), col(WR), 1, ["wr", "nb", "rc"], ["g0"], scale=col(NB), bias=col(RC))
+    for s in range(16):
+        mm(T.px[:, 0:8], T.w1[:, 15 - s:143 - s], T.xt[:, :, s:32:16], s == 0, s == 15, 8, ["w1"] + ["xt%d" % k for k in range(1, 8)], "px")
+    act(T.yt[:], T.px[:, 0:8], 8, (), ["yt"], ["px"])
+    tag[0] = "tr3"
+    mm(T.px[:, 0:256], T.idb[:], T.tc[:], True, False, 256, ["idb", "tc"], "px")
+    for t in range(2):
+        yq = lambda q: T.yt[:, 2 * q + t:2 * q + t + 1]
+        ts(T.mk[:, 16 + t, 0:256], T.tc[:], yq(0), yq(3), ALU.is_gt, ALU.add, 128, ["tc", "yt"], ["sa%d" % t])
+        ts(T.mk[:, 18 + t, 0:256], T.tc[:], yq(0), None, ALU.is_equal, None, 128, ["tc", "yt"], ["sb%d" % t])
+        act(T.mk[:, 20 + t, 0:128], T.bo[:], 128, ["bo", "yt"], ["sc%d" % t], scale=yq(2))
+        ts(T.mk[:, 22 + t, 0:128], T.rt[:], yq(1), yq(2), ALU.is_gt, ALU.mult, 64, ["rt", "yt"], ["sd%d" % t])
+        mm(T.px[:, 0:256], T.mk[:, 20 + t, 0:128], T.mk[:, 16 + t, 0:256], False, False, 256, ["sa%d" % t, "sc%d" % t], "px")
+        mm(T.px[:, 0:256], T.mk[:, 22 + t, 0:128], T.mk[:, 18 + t, 0:256], False, t == 1, 256, ["sb%d" % t, "sd%d" % t], "px")
+    ts(T.off3[:], T.px[:, 0:256], col(G0), None, ALU.add, None, 256, ["g0"], ["off3"], ["px"])
+    logs = ["ring"] + seven("log0_%d") + seven("log1_%d") + seven("log2_%d")
+    parts, tag[0] = [], "scale"
+    for c0, c1, q in CFG["scale"]:
+        parts.append("part%d" % c0)
+        if q == "s":
+            act(T.win[:, c0:c1], T.raw[:, c0:c1], c1 - c0, ["ring"], parts[-1:], scale=1.0 / 256)
+        else:
+            ts(T.win[:, c0:c1], T.raw[:, c0:c1], 1.0 / 256, None, ALU.mult, None, (c1 - c0) / 2, ["ring"], parts[-1:])
     for e in range(3):
-        packets(e, logs[:4 + e])
+        packets(e, logs[:1 + 7 * e] + (parts if e else []))
     tag[0] = "out"
     for i, (c0, c1, q) in enumerate(CFG["ych"]):
-        gather(q, T.yb[:, c0:c1], T.win[:], T.off3[:, c0 // 16:c1 // 16], c1 - c0, logs + ["off3"], ["yb%d" % i], 256.0)
-        dma("y", T.y[:, c0:c1], T.yb[:, c0:c1], "sty", ["yb%d" % i], ["st%d" % i], 2000.0 + 1.6 * (P - c0))
+        gather(q, T.yb[:, c0:c1], T.win[:], T.off3[:, c0 // 16:c1 // 16], c1 - c0, logs + parts + ["off3"], ["yb%d" % i],
+               256.0 if scaled else None)
+        dma("y", T.y[:, c0:c1], T.yb[:, c0:c1], "sty", ["yb%d" % i], ["st%d" % i], 1800.0 + 0.8 * (c1 - c0))
     tail = [(s, got[s]) for s in got]
     tail += [("ldh", 32), ("ldc", 16), ("ldd", 16), ("ldr", 16), ("ls", sent[0]), ("sty", 16 * (len(CFG["ych"]) + 1))]
     return ops, tail

import numpy as np
from concourse.bass import DstId, RemoteDMATransfer
from concourse.mybir import AluOpType, ActivationFunctionType

N, P, TT, CAP = 8, 4096, 256, 128
ALU = AluOpType
ACT = ActivationFunctionType
F32, BF, I32, U16, F16 = "float32", "bfloat16", "int32", "uint16", "float16"
CFG = {
    "sel": (("v", "v"), ("v", "v"), ("s", "s")),
    "pick": ("vv ssss sss vvv sss sss sss", "vv ssss sss sss sss sss sss", "vv ssss vvv sss sss sss v ss"),
    "mod": ((((0, 1), "one"), ((2, 3), "one"), ((4,), "one"), ((5,), "two"), ((6,), "two")),) * 3,
    "lots": ((0, 1, 2, 3), (4,), (5, 6)),
    "up": ("sssssss",) * 3,
    "small": ((0, 1, 6), (2, 3), (4, 5)),
    "lists": (((0, 1), (2, 3)), ((4, 5, 6),)),
    "scale": [],
    "ych": ((0, 768, "s"), (768, 1536, "v"), (1536, 2176, "s"), (2176, 2816, "v"), (2816, 3200, "s"), (3200, 3584, "v"),
            (3584, 3840, "s"), (3840, 4096, "v")),
    "send": 300.0, "lat": 1200.0, "row": 12.0, "first": 1500.0, "tries": 22000, "seed": 3, "pe": 0.65, "sync": 110.0,
    "fv": 48.0, "fs": 70.0, "cy": 0.88, "ga": 1.45,
    "parts": "sel0 flags sel0a sel0b hc sel1 hash0_0 hash0_4 r0 sel2 cnt hash1_0 tr1 r1 hash2_0 tr2 r2 last tr3 out tab scale",
    "due": {"end": 36000.0, "xfl0i": 4200, "xfl1i": 4500, "xfl2i": 4800, "tl0": 5900, "tl1": 6900, "tl2": 9800,
            "off0_0": 10600, "off0_4": 11400, "off1": 17100, "off2": 23900},
    "tl": "vvs", "halves": ((0, 4, "px"), (4, 7, "pd3")), "hash0": ((0, 4), (4, 7)),
    "cases": ((1.25, 1.0, 0.9, 1.0), (1.0, 1.4, 1.3, 1.5), (1.3, 1.4, 1.2, 2.0)), "slack": 300.0,
}
for _e, _t in enumerate((12000, 18600, 25400)):
    for _l in range(7):
        CFG["due"]["s%d_%di" % (_e, _l)] = _t + 500 * _l
QOFF = 1088.0
MAGIC = 3.0 * 2 ** 30


def sb(shape, d):
    return ("sbuf", [128] + shape, d)


SCRATCH = {
    "win": sb([P + 3 * 896], BF), "yb": sb([P], F32),
    "ga0": sb([21 * CAP], BF), "ga1": sb([21 * CAP], BF), "ga2": sb([21 * CAP], BF),
    "qh": sb([896], F16), "qf": sb([896], F32), "ou0": sb([896], BF), "ou1": sb([896], BF), "ou2": sb([896], BF),
    "hcr": sb([24], I32), "hcf": sb([24], F32), "hcs": sb([24], F32), "cami": sb([336], I32),
    "fo": sb([336], BF), "so": sb([352], BF), "pw0": sb([112], BF), "pwo": sb([224], BF), "pwr": sb([112], BF),
    "msk": sb([224], BF), "pi": sb([4], I32), "col": sb([24], F32),
    "ti": sb([144], BF), "tg": sb([128], BF), "tabr": sb([56], BF), "tab0": sb([56], BF), "tabl": sb([56], BF),
    "tabx": sb([56], BF), "half": sb([256], BF),
    "zf": sb([24], F32), "i896": sb([896], BF), "gt": sb([128], F32),
    "idb": sb([128], BF), "nid": sb([128], BF), "idh": sb([128], F16), "nq": sb([128], F16),
    "wm": sb([144], BF), "wh": sb([144], BF),
    "bo": sb([128], BF), "nbo": sb([128], BF), "lt": sb([128], BF), "gm": sb([8], BF), "gm15": sb([8], BF),
    "rw": sb([6, 8], BF), "dg": sb([6, 128], BF), "ids": sb([128], BF), "raw": sb([P], BF), "qi": sb([896], I32),
    "bq": sb([24], F32), "dl": sb([24], F32), "cd": sb([24], F32), "dj": sb([4], F32), "djr": sb([4], BF),
    "dja": sb([4], F32), "djb": sb([4], F32), "b2": sb([4], F32), "cc": sb([4], F32), "nw": sb([4], F32),
    "ct": sb([24], F32), "cm0": sb([8, 8, 16], BF), "cm1": sb([8, 8, 16], BF), "cm2": sb([8, 8, 16], BF),
    "of1": sb([168], U16), "c0": sb([896], BF), "c1": sb([896], BF), "c2": sb([896], BF), "g2": sb([896], BF),
    "tl": sb([112], F32), "xl": sb([112], F32), "cw": sb([168], BF),
    "ha0": sb([7, 3, 8], I32), "hb0": sb([7, 3, 8], I32), "ha1": sb([7, 3, 8], I32), "hb1": sb([7, 3, 8], I32),
    "ha2": sb([7, 3, 8], I32), "hb2": sb([7, 3, 8], I32),
    "off0": sb([168], U16), "off1": sb([168], U16), "off2": sb([168], U16), "off3": sb([256], U16),
    "jh": sb([336], F16), "mk": sb([24, 256], BF), "th": sb([3, 24], I32), "xt": sb([4, 32], BF), "yt": sb([8], F32),
    "tc": sb([256], BF), "ru": sb([128], BF), "rt": sb([128], BF), "w1": sb([144], BF),
}
for _b in ("pd0", "pd1", "pd2", "pd3", "pa", "pb", "px", "pq"):
    SCRATCH[_b] = ("psum", [128, 512], F32)
SEMAPHORES = ["cv", "cs", "cp", "cg", "ldh", "ldc", "ldd", "ldr", "sty", "ls", "fl", "li0", "li1", "li2", "a0", "a1", "a2",
              "b0", "b1", "b2", "c0", "c1", "c2"]
CNT = {"v": "cv", "s": "cs", "p": "cp", "g": "cg"}
SYNC = 110.0


def peers(T, topo, me):
    a = T.cores[me]

    def key(r):
        b = T.cores[r]
        ca, cb = topo.chip(a), topo.chip(b)
        far = 3 if ca == cb else 2 if topo.mates(ca, cb) else 1 if topo.same_plane(ca, cb) else 0
        return (far, topo.die(a) == topo.die(b), r)
    return sorted([r for r in range(N) if r != me], key=key)


def engines_for(T, topo, a, b):
    ca, cb = T.cores[a], T.cores[b]
    en = topo.engines(ca, cb)
    if topo.chip(ca) == topo.chip(cb):
        for c in T.cores:
            if topo.chip(c) != topo.chip(ca):
                en = [e for e in en if e not in topo.engines(ca, c)]
    return en


def one_pass(ops, before, topological, free, pr):
    pr = list(pr)
    for i in topological:
        for d, lag in before[i]:
            if pr[i] >= pr[d]:
                pr[i] = pr[d] - 1e-3
    seq = sorted(topological, key=lambda i: -pr[i])
    busy, end = dict((q, []) for q in "vspgyd"), [0.0] * len(ops)
    for j in seq:
        c, t = ops[j]["cost"], free[j]
        for d, lag in before[j]:
            if end[d] + lag > t:
                t = end[d] + lag
        if ops[j]["q"]:
            b = busy[ops[j]["q"]]
            k = len(b)
            while k and b[k - 1][1] > t:
                k -= 1
            while k < len(b) and b[k][0] < t + c:
                t = b[k][1]
                k += 1
            b.insert(k, (t, t + c))
        end[j] = t + c
    return seq, end


def plan(ops):
    n = len(ops)
    deps, kids = [[] for _ in range(n)], [[] for _ in range(n)]
    for i, o in enumerate(ops):
        for d in sorted(set(o["deps"] + o["ord"])):
            same = (ops[d]["q"] == "p" and o["q"] == "p") or d not in o["deps"]
            lag = 0.0 if same else ops[d]["lat"] + (CFG["sync"] if o["q"] and o["q"] != "d" else 0.0)
            deps[i].append((d, lag))
            kids[d].append((i, lag))
    zero, lat = [0.0] * n, [o["lat"] for o in ops]
    rs = np.random.RandomState(CFG["seed"])
    up, down = list(range(n)), list(reversed(range(n)))
    cases = []
    for fc, fg, fl, fd in CFG["cases"]:
        cost = [o["cost"] * (fd if o["q"] == "d" else fl if o["far"] else fg if "ind" in o else fc if o["q"] != "y" else 1.0)
                for o in ops]
        cases.append((cost, [[(d, lag * (fl if ops[d]["far"] else 1.0)) for d, lag in deps[i]] for i in range(n)]))

    def replay(order, cost, before):
        free, end = {}, [0.0] * n
        for j in order:
            t = free.get(ops[j]["q"], 0.0)
            for d, lag in before[j]:
                if end[d] + lag > t:
                    t = end[d] + lag
            end[j] = t + cost[j]
            if ops[j]["q"]:
                free[ops[j]["q"]] = end[j]
        return max([end[i] + lat[i] for i in range(n)])
    tags = sorted(set([o["tag"] for o in ops]))
    back = [0.0] * n
    for i in down:
        due = [CFG["due"][w] for w in ops[i]["w"] if w in CFG["due"]]
        back[i] = max([-CFG["due"]["end"] + lat[i]] + [-t for t in due] + [back[k] + ops[k]["cost"] + lag for k, lag in kids[i]])
    back = [back[i] + ops[i]["cost"] for i in range(n)]
    best = now = None
    for it in range(CFG["tries"] + 1):
        pr = list(back) if it % 2 == 0 or now is None else [-t for t in now[3]]
        if it % 5 == 4:
            tg, dv = tags[int(rs.randint(len(tags)))], float(rs.normal()) * 1500.0
            pr = [pr[i] + (dv if ops[i]["tag"] == tg else 0.0) for i in range(n)]
        else:
            for _ in range(1 + it % 3 if it > 3 else 0):
                k, dv = int(rs.randint(n)), float(rs.normal()) * 600.0
                for i in range(k, min(n, k + 1 + it % 9)):
                    pr[i] += dv
        seq, end = one_pass(ops, deps, up, zero, pr)
        t = max([end[i] + lat[i] for i in range(n)])
        if now is not None and t > now[1] * 1.02:
            continue
        pos = dict((j, k) for k, j in enumerate(seq))
        order = sorted(up, key=lambda i: (end[i] - ops[i]["cost"], pos[i]))
        ts = [t] + [replay(order, cost, before) for cost, before in cases]
        if now is None or sum(ts) <= now[0] + CFG["slack"] * (1.0 - it / CFG["tries"]):
            now = (sum(ts), t, order, end, ts)
            back = one_pass(ops, kids, down, lat, [end[i] + lat[i] for i in range(n)])[1]
            if best is None or now[0] < best[0]:
                best = now
    for i in range(n):
        ops[i]["t0"] = best[3][i] - ops[i]["cost"]
    CFG["est"] = best[4]
    return best[2]


def emit(g, T, ops, order, tail):
    eng = {"v": g.vector, "s": g.scalar, "p": g.tensor, "g": g, "y": g.sync}
    pos = dict((j, k) for k, j in enumerate(order))
    need = set()
    for j in order:
        o = ops[j]
        if o["q"] == "d":
            o["q"] = None
        if o["q"] and o["q"] != "p":
            ds = [d for d in o["deps"] if ops[d]["q"] == "p"]
            if ds:
                need.add(max(ds, key=lambda d: pos[d]))
    cnt = {"v": 0, "s": 0, "p": 0, "g": 0}
    nxt = None
    for j in order:
        o = ops[j]
        if o["sem"] is None and o["q"]:
            if o["q"] != "p" or j in need:
                cnt[o["q"]] += 1
                o["inc"] = True
            o["sig"] = (CNT[o["q"]], cnt[o["q"]])
    for j in reversed(order):
        o = ops[j]
        if o["q"] == "p":
            if o.get("inc"):
                nxt = o["sig"]
            else:
                o["sig"] = nxt
    known = dict((q, {}) for q in eng)
    for j in order:
        o = ops[j]
        q = o["q"]
        if not q:
            o["snap"] = {}
            continue
        k = known[q]
        for d in sorted(o["deps"], key=lambda d: -pos[d]):
            od = ops[d]
            if (q == "p" and od["q"] == "p") or od["sem"] == "none":
                continue
            s, v = od["sem"] if od["sem"] else od["sig"]
            if k.get(s, 0) < v:
                eng[q].wait_ge(T.sem[s], v)
                k[s] = v
            for s2, v2 in od["snap"].items():
                if k.get(s2, 0) < v2:
                    k[s2] = v2
        o["snap"] = dict(k)
        ins = o["fn"](eng[q])
        if o.get("inc"):
            ins.then_inc(T.sem[CNT[q]], 1)
    for q in cnt:
        g.wait_ge(T.sem[CNT[q]], cnt[q])
    for s, v in tail:
        g.wait_ge(T.sem[s], v)


def build(T, topo, me):
    ops, lastw, readers, tag, before = [], {}, {}, ["tab"], {}

    def add(q, fn, r=(), w=(), x=(), cost=0.0, lat=0.0, sem=None):
        deps = set()
        for k in list(r) + list(x) + list(w):
            if k in lastw:
                deps.add(lastw[k])
        for k in w:
            deps.update(readers.get(k, []))
        for k in x:
            deps.update([i for i in readers.get(k, []) if ops[i]["q"] != q])
        i = len(ops)
        ops.append({"q": q, "fn": fn, "deps": sorted(deps), "cost": cost, "lat": lat, "sem": sem, "w": list(w),
                    "tag": tag[0], "ord": [], "far": q == "g" and sem == "none"})
        part = (tag[0][:3] if tag[0][:2] == "ou" else tag[0], q, w[0][:2] if tag[0][:2] == "ou" and q in ("v", "s") else "")
        if q and tag[0] != "tab" and part in before:
            ops[i]["ord"].append(before[part])
        before[part] = i
        for k in list(r) + list(x):
            readers.setdefault(k, []).append(i)
        for k in w:
            lastw[k] = i
            readers[k] = []

    def vc(n):
        return CFG["fv"] + CFG["cy"] * max(64.0, n)

    def ts(out, a, s1, s2, o0, o1, n, r, w, x=()):
        if o1 is None:
            add("v", lambda e: e.tensor_scalar(out, a, s1, None, o0), r, w, x, vc(n))
        else:
            add("v", lambda e: e.tensor_scalar(out, a, s1, s2, o0, o1), r, w, x, vc(n))

    def tt(out, a, b, o, n, r, w, x=()):
        add("v", lambda e: e.tensor_tensor(out, a, b, o), r, w, x, vc(n))

    def cp(out, a, n, r, w, x=()):
        add("v", lambda e: e.tensor_copy(out, a), r, w, x, vc(n))

    def ms(out, v, n, w):
        add("v", lambda e: e.memset(out, v), (), w, (), vc(n))

    def scan(out, a, b, init, o0, o1, n, r, w, x=()):
        add("v", lambda e: e.tensor_tensor_scan(out, a, b, init, o0, o1), r, w, x, vc(n))

    def act(out, a, n, r, w, x=(), fn=ACT.Identity, **kw):
        add("s", lambda e: e.activation(out, a, fn, **kw), r, w, x, CFG["fs"] + CFG["cy"] * max(64.0, n))

    def mm(out, lt, rh, st, sp, n, r, bank):
        add("p", lambda e: e.matmul(out, lt, rh, st, sp), r, [bank], (), CFG["pe"] * max(64.0, n), 60.0)

    def iota(out, pat, base, cm, n, w, flag=True):
        if flag:
            add("g", lambda e: e.iota(out, pat, base, cm, allow_small_or_imprecise_dtypes=True), (), w, (), 150.0 + 1.7 * n)
        else:
            add("g", lambda e: e.iota(out, pat, base, cm), (), w, (), 150.0 + 1.7 * n)

    def gather(q, out, win, off, n, r, w, scale=None):
        if q == "s":
            add("s", lambda e: e.activation(out, win.indirect(off), ACT.Identity, scale=scale or 1.0), r, w, (), CFG["fs"] + CFG["ga"] * n)
        elif scale:
            add("v", lambda e: e.tensor_scalar(out, win.indirect(off), scale, None, ALU.mult), r, w, (), CFG["fv"] + CFG["ga"] * n)
        else:
            add("v", lambda e: e.tensor_copy(out, win.indirect(off)), r, w, (), CFG["fv"] + CFG["ga"] * n)
        ops[-1]["ind"] = True

    def dma(q, out, a, sem, r, w, lat=0.0):
        add(q, lambda e: e.dma_start(out, a).then_inc(T.sem[sem], 16), r, w, (), 60.0, lat, "none")

    def event(sem, v, r, w, lat):
        add(None, None, r, w, (), 0.0, lat, (sem, v))

    order = peers(T, topo, me)
    back = [peers(T, topo, r).index(me) for r in order]
    dto = [(me - r) % N for r in order]
    dfrom = [(r - me) % N for r in order]
    sent, got = [0], {}

    def send(ls, outs, ins, sem, rd, w, nb):
        trs = []
        for l, o, a in zip(ls, outs, ins):
            en = engines_for(T, topo, me, order[l])
            share = [x for x in ls if engines_for(T, topo, me, order[x]) == en]
            k = len(en) // len(share)
            while k & (k - 1):
                k -= 1
            mine = en[share.index(l) * k:(share.index(l) + 1) * k]
            ad = topo.addr(T.cores[order[l]])
            trs.append((o, a, ad, sum([1 << x for x in mine])))
            sent[0] += k
            got[sem] = got.get(sem, 0) + k
        s = T.sem[sem]
        if len(trs) == 1:
            o, a, ad, m = trs[0]
            add("g", lambda e: e.remote_dma(o, a, s, T.sem.ls, ad[1], ad[0], m), rd, [w + "i"], (), CFG["send"],
                CFG["lat"], "none")
        else:
            tr = [RemoteDMATransfer(dst_ids=[DstId(rid=ad[0], pnc=ad[1])], dma_engine_mask=m, remote_sem=s, src=a, dst=o)
                  for o, a, ad, m in trs]
            add("g", lambda e: e.remote_dma_fused(tr, local_sem=T.sem.ls), rd, [w + "i"], (), CFG["send"],
                CFG["lat"], "none")
        far = len([l for l in ls if topo.chip(T.cores[order[l]]) != topo.chip(T.cores[me])])
        t = 128 / min([bin(m).count("1") for o, a, ad, m in trs]) * (CFG["row"] + nb / 25.0)
        add("d" if far else None, None, [w + "i"], [w], (), t if far else 0.0, 0.0 if far else t, "none")

    def exchange(calls, out, a, sem, rd, w, nb, lat):
        for i, ls in enumerate(calls):
            send(ls, [out(l) for l in ls], [a(l) for l in ls], sem, rd, "x%s%d" % (sem, i), nb)
        event(sem, got[sem], ["x%s%d" % (sem, i) for i in range(len(calls))], w, lat)

    col = lambda k: T.col[:, k:k + 1]
    PC, GC, G16, W15, SN, M0, M4, MA, MB, H2, NA, NB, WR, Z0, Z1, G0, RC, S1 = range(18)
    R0, R1 = range(2)
    hcs = lambda k: T.hcs[:, k:k + 1]
    seven = lambda s: [s % l for l in range(7)]

    dma("y", T.cami[:, 0:112], T.came[:, 0:112], "ldc", (), ["l0"])
    dma("s", T.cami[:, 112:336], T.came[:, 112:336], "ldd", (), ["l3"])
    dma("y", T.hcr[0:8, 0:21], T.hc[:], "ldh", ["l0"], ["l1"])
    dma("s", T.hcr[0:8, 21:22], T.had[:], "ldh", ["l3"], ["l2"])
    scaled = len(CFG["scale"]) > 0
    dma("y", T.raw[:] if scaled else T.win[:, 0:P], T.ring[:], "ldr", ["l1"], ["l4"])
    event("ldh", 32, ["l1", "l2"], ["hcr"], 2100.0)
    event("ldc", 16, ["l0"], ["cami0"], 2100.0)
    event("ldd", 16, ["l3"], ["cami1"], 2300.0)
    event("ldr", 16, ["l4"], ["ring"], 4500.0)

    iota(T.pi[:, 0:1], [[0, 1]], 0, 1, 1, ["pi"], False)
    iota(T.tg[:], [[1, 8], [0, 16]], 0, 0, 128, ["tg"])
    iota(T.ti[:], [[1, 144]], 0, 0, 144, ["ti"])
    iota(T.tabl[:], [[16, 7], [0, 8]], 0, 0, 56, ["tabl"])
    iota(T.tc[:], [[16, 256]], 0, 0, 256, ["tc"])
    iota(T.ru[:], [[0, 8], [1, 16]], 1, 0, 128, ["ru"])
    ms(T.msk[:], 1.0, 112, ["msk"])
    ms(T.msk[:, 0:224:16], 0.0, 14, ["msk"])
    act(T.zf[:], T.msk[:, 0:24], 24, ["msk"], ["zf"], scale=0.0)
    act(T.xt[:], T.msk[:, 0:128], 128, ["msk"], ["xt0"], scale=0.0)
    act(T.so[:, 336:352], T.msk[:, 0:16], 16, ["msk"], ["soz"], scale=0.0)
    act(T.bq[:, 22:24], T.msk[:, 0:2], 2, ["msk"], ["bq0"], scale=0.0, bias=-2048.0)
    for l, r in enumerate(order):
        act(T.tab0[:, 8 * l:8 * l + 8], T.msk[:, 0:8], 8, ["msk"], ["tab0%d" % l], scale=0.0, bias=16.0 * (dfrom[l] - 1))
        iota(T.tabr[:, 8 * l:8 * l + 8], [[0, 8]], TT * (r - l), 0, 8, ["tabr%d" % l])
    cp(col(PC), T.pi[:, 0:1], 1, ["pi"], ["pc"])
    ts(T.pi[:, 1:2], T.pi[:, 0:1], 4, None, ALU.arith_shift_right, None, 1, ["pi"], ["gi"])
    cp(col(GC), T.pi[:, 1:2], 1, ["gi"], ["gc"])
    act(col(G16), col(GC), 1, ["gc"], ["g16"], scale=16.0)
    ts(col(W15), T.pi[:, 1:2], 16.0, 15.0, ALU.mult, ALU.add, 1, ["gi"], ["w15"])
    ts(col(SN), col(PC), col(W15), None, ALU.not_equal, None, 1, ["pc", "w15"], ["sn"])
    ts(T.gt[0:8, :], T.tg[0:8, :], T.col[0:8, PC:PC + 1], None, ALU.is_equal, None, 128, ["tg", "pc"], ["gt"])
    ts(T.idb[:], T.ti[:, 0:128], col(PC), None, ALU.is_equal, None, 64, ["ti", "pc"], ["idb"])
    ts(T.idh[:], T.ti[:, 0:128], col(PC), None, ALU.is_equal, None, 64, ["ti", "pc"], ["idh"])
    hows = [how for m in CFG["mod"] for ls, how in m]
    if "one" in hows:
        act(T.ids[:], T.idb[:], 128, ["idb"], ["ids"], scale=1.0 / 256)
    if "two" in hows:
        ms(T.half[:, 0:128], -127.5, 64, ["half"])
    if "s" in hows or "v" in hows:
        ts(T.nq[:], T.ti[:, 0:128], col(PC), -256.0, ALU.is_equal, ALU.mult, 64, ["ti", "pc"], ["nq"])
    ts(T.wm[:], T.ti[:], col(W15), None, ALU.is_equal, None, 72, ["ti", "w15"], ["wm"])
    ts(T.bo[:], T.tg[:], col(GC), None, ALU.is_equal, None, 64, ["tg", "gc"], ["bo"])
    ts(T.rw[:, R0, 0:7], T.tab0[:, 0:56:8], col(G16), col(SN), ALU.is_equal, ALU.mult, 8, seven("tab0%d") + ["g16", "sn"], ["r0"])
    act(T.rw[:, R1, :], T.bo[:, 0:128:16], 8, ["bo", "sn"], ["r1"], scale=col(SN))
    for k in set([(R0, R0, R1)[z] for z in range(3) if CFG["sel"][z][0] == "s"]):
        act(T.rw[:, k + 2, 0:7], T.rw[:, k, 0:7], 8, ["r%d" % k], ["r%d" % (k + 2)], scale=0.5)
    act(T.tabx[:], T.tab0[:], 56, seven("tab0%d"), ["tabx"], scale=-16.0, bias=float(TT * me))
    act(T.wh[:], T.wm[:], 144, ["wm"], ["wh"], scale=0.5)
    act(col(S1), col(SN), 1, ["sn"], ["s1"], scale=-1.0, bias=1.0)
    act(T.w1[:], T.wm[:], 144, ["wm", "s1"], ["w1"], scale=col(S1))
    act(col(RC), col(G16), 1, ["g16", "pc"], ["rc"], scale=-1.0, bias=col(PC))
    add("g", lambda e: e.affine_select(T.rt[:], T.ru[:], [[-16, 8], [0, 16]], ALU.is_ge, 0.0, 0, 1), ["ru"], ["rt0"], (), 400.0)
    add("g", lambda e: e.affine_select(T.rt[:], T.rt[:], [[16, 8], [0, 16]], ALU.is_ge, 0.0, 15, -1), ["rt0"], ["rt"], (), 400.0)
    act(T.nid[:], T.idb[:], 128, ["idb"], ["nid"], scale=-1.0)
    act(T.nbo[:], T.bo[:], 128, ["bo"], ["nbo"], scale=-1.0)
    add("g", lambda e: e.affine_select(T.lt[:], T.nbo[:], [[-1, 128]], ALU.is_gt, 0.0, 0, 1), ["nbo"], ["lt"], (), 450.0)
    iota(T.i896[:, 0:512], [[0, 4], [1, 128]], 0, 0, 512, ["i896_0"])
    act(T.i896[:, 512:896], T.i896[:, 0:384], 384, ["i896_0"], ["i896_1"])
    I896 = ["i896_0", "i896_1"]

    tag[0] = "hc"
    ts(T.hcr[0:8, 22:23], T.hcr[0:8, 21:22], P - 1, None, ALU.bitwise_and, None, 1, ["hcr"], ["hcm"])
    cp(T.hcf[0:8, 0:23], T.hcr[0:8, 0:23], 23, ["hcr", "hcm"], ["hcf"])
    mm(T.pq[:, 0:23], T.gt[0:8, :], T.hcf[0:8, 0:23], True, True, 256, ["gt", "hcf"], "pq")
    act(T.hcs[:, 0:23], T.pq[:, 0:23], 23, (), ["hcs"], ["pq"])
    ts(T.cc[:, 0:1], hcs(21), float(P), 1.0 / P, ALU.min, ALU.mult, 1, ["hcs"], ["cc0"])
    for k in range(3):
        act(T.dg[:, k, :], T.idb[:], 128, ["idb", "hcs"], ["dg%d" % k], scale=hcs(18 + k))
        if "one" in hows:
            act(T.dg[:, 3 + k, :], T.ids[:], 128, ["ids", "hcs"], ["dg%d" % (3 + k)], scale=hcs(18 + k))

    def hashes(e, l0, l1, xs, xr, xx, bank):
        tag[0] = "hash%d_%d" % (e, l0)
        ha, hb = T["ha%d" % e], T["hb%d" % e]
        n, c0 = (l1 - l0) * 24, l0 * 24
        ka, kb = "ha%d_%d" % (e, l0), "hb%d_%d" % (e, l0)
        a, b, pq = ha[:, l0:l1], hb[:, l0:l1], T[bank][:, 0:n]
        kk = [ka + "k%d" % k for k in range(3)]
        for k in range(3):
            ts(ha[:, l0:l1, k, :], xs, hcs(6 * e + k), hcs(6 * e + 3 + k), ALU.mult, ALU.add, n / 3, ["hcs"] + xr, [kk[k]], xx)
        ts(b, a, P - 1, None, ALU.bitwise_and, None, n, kk, [kb])
        ts(pq, b, 2.0, float(P - 1), ALU.mult, ALU.subtract, n, [kb], [bank])
        tt(a, b, pq, ALU.mult, n, [kb], [ka] + kk, [bank])
        ts(b, a, P - 1, None, ALU.bitwise_and, None, n, [ka], [kb])
        if e == 0:
            ts(a, b, T.cc[:, 0:1], 2047.5 - 2.0 ** -13, ALU.mult, ALU.subtract, n, [kb, "cc0"], [ka])
            ts(T.off0[:, c0:c0 + n], a, 2047.0, None, ALU.add, None, n, [ka], ["off0_%d" % l for l in range(l0, l1)])
        else:
            ts(a, b, T.cc[:, e:e + 1], col(M4), ALU.mult, ALU.subtract, n, [kb, "cc12", "m4"], [ka])
            ts(b, a, 12, P - 1, ALU.arith_shift_right, ALU.bitwise_and, n, [ka], [kb])
            translate(e, b, kb, n, bank)

    def translate(e, j, kj, n, bank):
        L, tag[0] = 7 * e, "tr%d" % e
        s0, m0 = 168 * (e - 1), 0
        jh, acc, kh = T.jh[:, s0:s0 + n], T[bank][:, 0:n], "jh%d" % e
        ts(jh, j, 2048.0, None, ALU.subtract, None, n, [kj], [kh])
        mm(acc, T.idh[:], jh, True, False, n, ["idh", kh], bank)
        steps = [(T.bq[:, i:i + 1], T.dl[:, i:i + 1]) for i in range(L - 1)]
        steps += [(T.bq[:, L - 1:L], T.dja[:, e - 1:e]), (T.bq[:, L - 1:L], T.djb[:, e - 1:e]), (T.b2[:, e - 1:e], -float(P))]
        for i, (b, d) in enumerate(steps):
            km = "mk%d_%d" % (i, m0)
            ts(T.mk[:, i, m0:m0 + n], jh, b, d, ALU.is_ge, ALU.mult, n / 2, [kh, "bq", "dl", "dja", "djb", "b2"], [km])
            mm(acc, T.idb[:], T.mk[:, i, m0:m0 + n], False, i == len(steps) - 1, n, ["idb", km], bank)
        ts(T["off%d" % e][:], acc, float(P + 2048), None, ALU.add, None, n, (), ["off%d" % e], [bank])

    def select(z, tot, ktot, gm, pw, kpw, tab, ba, bd, parts):
        (u1, u2), tag[0] = CFG["sel"][z], "sel%d" % z
        cm, c2, A = T["cm%d" % z], T["c%d" % z], T[ba]
        ra = (R0 if z < 2 else R1) + (0 if u1 == "v" else 2)
        kr = ["r%d" % ra]
        mm(A[0:112, 112:120], tot, gm, True, True, 8, ["bo", "idb"] + ktot, ba)
        if u1 == "s":
            act(T.ct[0:112, 8 * z:8 * z + 8], A[0:112, 112:120], 8, (), ["ct%d" % z], [ba], scale=-1.0, bias=0.5)
        kc = ["cm%d_%d" % (z, a) for a in range(8)]
        for a in range(8):
            if u1 == "v":
                ts(cm[0:112, :, a, :], T.ti[0:112, 0:128], A[0:112, 112 + a:113 + a], None, ALU.is_ge, None, 64, ["ti"],
                   [kc[a]], [ba])
            else:
                act(cm[0:112, :, a, :], T.ti[0:112, 0:128], 128, ["ti", "ct%d" % z], [kc[a]], fn=ACT.Sign,
                    bias=T.ct[0:112, 8 * z + a:8 * z + a + 1])
        mm(A[:, 128:184], T.idb[:], tab[:], True, False, 56, ["idb", "tabl"] + seven("tab0%d"), ba)
        for a in range(8):
            mm(A[:, 128 + a:184:8], cm[0:112, a], T.rw[0:112, ra, 0:7], False, a == 7, 7, kc + kr, ba)
        ts(T.of1[:, 56 * z:56 * z + 56], A[:, 128:184], 0.0 if u1 == "v" else 7.5, None, ALU.add, None, 56, (),
           ["of1%d" % z], [ba])
        act(T.cw[:, 56 * z:56 * z + 56], A[:, 128:184], 56, (), ["cw%d" % z], [ba], scale=16.0,
            bias=120.0 * (u1 == "s") + 8.0 * (u2 == "s"))
        for l0, l1, bx in parts:
            tag[0] = "sel%d" % z + ("" if z else "b" if l0 else "a")
            mm(T[bx][:, 0:8 * (l1 - l0)], T.idb[:], (T.tabr if z == 2 else T.tabx)[:, 8 * l0:8 * l1], True, False, 56,
               ["idb"] + (seven("tabr%d") if z == 2 else ["tabx"]), bx)
            mm(T[bx][:, 0:8 * (l1 - l0)], T.idb[:], T.cw[:, 56 * z + 8 * l0:56 * z + 8 * l1], False, False, 56,
               ["idb", "cw%d" % z], bx)
        for h, (l0, l1) in enumerate(((0, 4), (4, 7))):
            c0, c1, oh = CAP * l0, CAP * l1, T.of1[:, 56 * z + 8 * l0:56 * z + 8 * l1]
            kh, tag[0] = "c%d_%d" % (z, h), "sel%d" % z + ("" if z else "ab"[h])
            if u2 == "v":
                add("v", lambda e, c0=c0, c1=c1, oh=oh: e.tensor_tensor(c2[:, c0:c1], pw.indirect(oh), T.i896[:, c0:c1], ALU.is_le),
                    kpw + ["of1%d" % z] + I896, [kh], (), CFG["fv"] + CFG["ga"] * (c1 - c0))
                ops[-1]["ind"] = True
            else:
                D = T[bd[h]][:, 0:c1 - c0]
                gather("s", T.g2[:, c0:c1], pw, oh, c1 - c0, kpw + ["of1%d" % z], ["g2_%d" % h])
                mm(D, T.idb[:], T.i896[:, c0:c1], True, False, c1 - c0, ["idb"] + I896, bd[h])
                mm(D, T.nid[:], T.g2[:, c0:c1], False, True, c1 - c0, ["nid", "g2_%d" % h], bd[h])
        for h, (l0, l1) in enumerate(((0, 4), (4, 7))):
            c0, c1 = CAP * l0, CAP * l1
            if u2 == "s":
                act(c2[:, c0:c1], T[bd[h]][:, 0:c1 - c0], c1 - c0, (), ["c%d_%d" % (z, h)], [bd[h]], fn=ACT.Sign, bias=0.5)
        for l0, l1, bx in parts:
            tag[0] = "sel%d" % z + ("" if z else "b" if l0 else "a")
            for s in range(16):
                mm(T[bx][:, 0:8 * (l1 - l0)], (T.wm if u2 == "v" else T.wh)[:, 15 - s:143 - s], c2[:, CAP * l0 + s:CAP * l1:16],
                   False, s == 15, 56, ["wm", "wh"] + ["c%d_%d" % (z, h) for h in range(2) if l0 < (4, 7)[h] and l1 > (0, 4)[h]], bx)

    def packets(e, wkeys):
        n = CAP
        ga, ou, off = T["ga%d" % e], T["ou%d" % e], T["off%d" % e]
        win = T.raw[:] if scaled and e == 0 else T.win[:, 0:P + 896 * e]
        last, banks = {}, [0]
        u0 = 0
        for run in CFG["pick"][e].split():
            q, u1 = run[0], u0 + len(run)
            tag[0] = "ga%d_%d" % (e, u0 // 3)
            gather(q, ga[:, u0 * n:u1 * n], win, off[:, u0 * 8:u1 * 8], (u1 - u0) * n,
                   wkeys + (["off0_%d" % (u // 3) for u in range(u0, u1)] if e == 0 else ["off%d" % e]),
                   ["ga%d_%d" % (e, u) for u in range(u0, u1)])
            if q in last:
                ops[-1]["ord"].append(last[q])
            last[q], u0 = len(ops) - 1, u1

        def weighted(ls, first, stop=True, low=False):
            bank = "pd%d" % (banks[0] % 4)
            banks[0] += 1
            ps = T[bank][:, 0:n * len(ls)]
            for i, l in enumerate(ls):
                part = T[bank][:, n * i:n * i + n]
                if first is not None:
                    mm(part, T.idb[:], first, True, False, n, ["idb", "half"], bank)
                for k in range(3):
                    kd, u = k + (3 if low else 0), 3 * l + k
                    mm(part, T.dg[:, kd, :], ga[:, n * u:n * u + n], k == 0 and first is None, k == 2 and stop, n,
                       ["dg%d" % kd, "ga%d_%d" % (e, u)], bank)
                if not stop:
                    mm(part, T.nq[:], T.qh[:, n * l:n * l + n], False, True, n, ["nq", "qq%d" % l], bank)
            return bank, ps
        for ls, how in CFG["mod"][e]:
            tag[0] = "ou%d_%d" % (e, ls[0])
            c0, c1, w = n * ls[0], n * ls[-1] + n, n * len(ls)
            ko, kq = ["ou%d_%d" % (e, l) for l in ls], ["qq%d" % l for l in ls]
            if how == "one":
                bank, ps = weighted(ls, None, True, e == 0 or not scaled)
                ts(T.qi[:, c0:c1], ps, 127.5 / 256, None, ALU.subtract, None, w, (), kq, [bank])
                tt(ou[:, c0:c1], ps, T.qi[:, c0:c1], ALU.subtract, w, kq, ko, [bank])
            elif how == "two":
                bank, ps = weighted(ls, T.half[:, 0:n])
                bank2, ps2 = weighted(ls, None)
                ts(T.qf[:, c0:c1], ps, MAGIC, MAGIC, ALU.add, ALU.subtract, w, (), kq, [bank])
                tt(ou[:, c0:c1], ps2, T.qf[:, c0:c1], ALU.subtract, w, kq, ko, [bank2])
            else:
                bank, ps = weighted(ls, None)
                ts(T.qh[:, c0:c1], ps, 1.0 / 256, QOFF - 127.5 / 256, ALU.mult, ALU.add, w, (), kq, [bank])
                bank, ps = weighted(ls, None, False)
                if how == "s":
                    act(ou[:, c0:c1], ps, w, (), ko, [bank], bias=256.0 * QOFF)
                else:
                    ts(ou[:, c0:c1], ps, 256.0 * QOFF, None, ALU.add, None, w, (), ko, [bank])
        small = [l for ls, how in CFG["mod"][e] for l in ls if how == "one" and not scaled]
        for i, ls in enumerate(CFG["lots"]):
            sem = "%s%d" % ("abc"[i], e)
            for l in ls:
                tag[0] = "ou%d_%d" % (e, l)
                send([l], [T.win[:, P + 896 * e + (dto[l] - 1) * n:P + 896 * e + dto[l] * n]], [ou[:, l * n:(l + 1) * n]],
                     sem, ["ou%d_%d" % (e, l)], "s%d_%d" % (e, l), 2 * n)
            event(sem, got[sem], ["s%d_%d" % (e, l) for l in ls], ["log%d_%d" % (e, l) for l in ls], 200.0)
            for l in ls:
                if l in small:
                    seg = T.win[:, P + 896 * e + (dfrom[l] - 1) * n:P + 896 * e + dfrom[l] * n]
                    if CFG["up"][e][l] == "s":
                        act(seg, seg, n, (), ["log%d_%d" % (e, l)], scale=256.0)
                    else:
                        ts(seg, seg, 256.0, None, ALU.mult, None, n / 2, (), ["log%d_%d" % (e, l)])

    for z, c0, c1, bank in ((0, 0, 112, "pb"), (1, 112, 336, "pd2")):
        tag[0], w = ("sel0", "flags")[z], c1 - c0
        cp(T.fo[:, c0:c1], T.cami[:, c0:c1], w, ["cami%d" % z], ["fo%d" % z])
        scan(T.so[:, c0:c1], T.msk[:, 0:w], T.fo[:, c0:c1], 0.0, ALU.mult, ALU.add, w / 2, ["fo%d" % z, "msk"], ["so%d" % z])
        mm(T[bank][:, 0:w], T.bo[:], T.so[:, c0:c1], True, False, w, ["bo", "so%d" % z], bank)
        mm(T[bank][:, 0:w], T.lt[:], T.fo[:, c0:c1], False, True, w, ["lt", "fo%d" % z], bank)
    tag[0] = "sel0"
    act(T.pw0[:], T.pb[:, 0:112], 112, (), ["pw0"], ["pb"])
    tag[0] = "flags"
    act(T.pwo[:], T.pd2[:, 0:224], 224, (), ["pwo"], ["pd2"])
    exchange(CFG["small"], lambda l: T.pwr[:, 16 * back[l]:16 * back[l] + 16],
             lambda l: T.pwo[:, 96 + 16 * dfrom[l]:112 + 16 * dfrom[l]], "fl", ["pwo"], ["pwr"], 32, CFG["first"])

    def lists(h, z, l0, l1, bx, calls):
        c = 56 * z
        (cp if CFG["tl"][h] == "v" else act)(T.tl[:, c + 8 * l0:c + 8 * l1], T[bx][:, 0:8 * (l1 - l0)], 56, (), ["tl%d" % h], [bx])
        exchange(calls, lambda l: T.xl[:, c + 8 * back[l]:c + 8 * back[l] + 8], lambda l: T.tl[:, c + 8 * l:c + 8 * l + 8],
                 "li%d" % h, ["tl%d" % h], ["xl%d" % h], 32, 200.0)
    halves = CFG["halves"]
    select(0, T.so[:, 0:112], ["so0"], T.bo[:, 0:128:16], T.pw0[:], ["pw0"], T.tab0, "pa", None, halves)
    for h, (l0, l1, bx) in enumerate(halves):
        tag[0] = "sel0" + "ab"[h]
        lists(h, 0, l0, l1, bx, CFG["lists"][h])
    select(1, T.so[:, 112:224], ["so1"], T.bo[:, 0:128:16], T.pwo[:, 0:112], ["pwo"], T.tab0, "pd1", ("pd2", "pa"), ((0, 7, "pb"),))
    lists(2, 1, 0, 7, "pb", CFG["small"])
    tag[0] = "cnt"
    mm(T.pq[:, 32:54], T.bo[:], T.so[:, 15:352:16], True, True, 22, ["bo", "so0", "so1", "soz"], "pq")
    scan(T.bq[:, 0:22], T.pq[:, 32:54], T.zf[:, 0:22], -2048.0, ALU.add, ALU.add, 22, ["zf"], ["bq"], ["pq"])
    act(T.dl[:, 0:21], T.pq[:, 32:53], 21, (), ["dl"], ["pq"], scale=-1.0, bias=float(CAP))
    scan(T.cd[:, 0:21], T.dl[:, 0:21], T.zf[:, 0:21], 0.0, ALU.add, ALU.add, 21, ["zf", "dl"], ["cd"])
    act(col(M4), hcs(22), 1, ["hcs"], ["m4"], scale=float(P))
    act(col(MA), hcs(22), 1, ["hcs"], ["ma"], bias=-float(P))
    act(col(MB), hcs(22), 1, ["hcs"], ["mb"], scale=-1.0, bias=2048.0)
    act(col(M0), hcs(22), 1, ["hcs"], ["m0"], bias=2048.0)
    act(col(NA), hcs(22), 1, ["hcs"], ["na"], scale=-1.0, bias=float(P))
    act(col(NB), hcs(22), 1, ["hcs"], ["nb"], scale=-1.0, bias=2.0 * P)
    act(col(H2), hcs(21), 1, ["hcs"], ["h2"], bias=2048.0)
    act(T.dj[:, 0:3], T.cd[:, 5:21:7], 3, ["cd", "ma"], ["dj"], scale=-1.0, bias=col(MA))
    act(T.djr[:, 0:3], T.dj[:, 0:3], 3, ["dj"], ["djr"])
    act(T.dja[:, 0:3], T.djr[:, 0:3], 3, ["djr"], ["dja"])
    tt(T.djb[:, 0:3], T.dj[:, 0:3], T.djr[:, 0:3], ALU.subtract, 6, ["dj", "djr"], ["djb"])
    ts(T.b2[:, 0:3], T.bq[:, 6:21:7], col(MB), None, ALU.max, None, 3, ["bq", "mb"], ["b2"])
    ts(T.cc[:, 1:3], T.bq[:, 6:14:7], col(H2), float(P), ALU.add, ALU.min, 2, ["bq", "h2"], ["cc12"])
    act(T.nw[:, 0:1], T.bq[:, 20:21], 1, ["bq", "h2"], ["nw"], bias=col(H2))
    dma("y", T.now[:], T.nw[0:128:16, 0:1], "sty", ["nw"], ["now"], 2000.0)

    for h, (l0, l1) in enumerate(CFG["hash0"]):
        hashes(0, l0, l1, T.xl[:, 8 * l0:8 * l1], ["xl%d" % i for i, x in enumerate(halves) if x[0] < l1 and x[1] > l0], [], "pd%d" % h)
    hashes(1, 0, 7, T.xl[:, 56:112], ["xl2"], [], "pa")
    select(2, T.pwr[:], ["pwr"], T.idb[:, 15:128:16], T.pwr[:], ["pwr"], T.tabl, "px", ("px", "pb"), ((0, 7, "pq"),))
    hashes(2, 0, 7, T.pq[:, 0:56], [], ["pq"], "pb")
    tag[0] = "last"
    xq = lambda q, a, b: T.xt[:, q, a:b]
    ts(T.th[:, 2, :], T.bq[:, 0:24], col(M0), None, ALU.add, None, 24, ["bq", "bq0", "m0"], ["th"])
    ts(T.th[:, 0, :], T.th[:, 2, :], P - 16, None, ALU.bitwise_and, None, 24, ["th"], ["thh"])
    ts(T.th[:, 1, :], T.th[:, 2, :], 15, None, ALU.bitwise_and, None, 24, ["th"], ["thl"])
    cp(T.xt[:, 0:2, 0:24], T.th[:, 0:2, :], 48, ["thh", "thl", "xt0"], ["xt1"])
    ts(col(WR), T.th[:, 2, 20:21], float(P), None, ALU.is_ge, None, 1, ["th"], ["wr"])
    ts(xq(3, 0, 20), T.th[:, 2, 0:20], float(P), col(WR), ALU.is_lt, ALU.mult, 20, ["th", "wr", "xt0"], ["xt2"])
    act(xq(2, 0, 20), T.dl[:, 0:20], 20, ["dl", "xt0"], ["xt3"])
    act(col(Z0), col(WR), 1, ["wr", "ma"], ["z0"], scale=-float(P), bias=col(MA))
    act(col(Z1), T.cd[:, 19:20], 1, ["cd", "z0"], ["z1"], scale=-1.0, bias=col(Z0))
    act(xq(2, 20, 21), col(Z1), 1, ["z1", "xt0"], ["xt4"])
    act(xq(2, 21, 22), xq(2, 20, 21), 1, ["z1", "xt4"], ["xt5"], scale=-1.0, bias=col(Z1))
    act(xq(2, 22, 23), col(NA), 1, ["na", "xt0"], ["xt6"])
    act(xq(2, 23, 24), xq(2, 22, 23), 1, ["na", "xt6"], ["xt7"], scale=-1.0, bias=col(NA))
    act(col(G0), col(WR), 1, ["wr", "nb", "rc"], ["g0"], scale=col(NB), bias=col(RC))
    for s in range(16):
        mm(T.px[:, 0:8], T.w1[:, 15 - s:143 - s], T.xt[:, :, s:32:16], s == 0, s == 15, 8, ["w1"] + ["xt%d" % k for k in range(1, 8)], "px")
    act(T.yt[:], T.px[:, 0:8], 8, (), ["yt"], ["px"])
    tag[0] = "tr3"
    mm(T.px[:, 0:256], T.idb[:], T.tc[:], True, False, 256, ["idb", "tc"], "px")
    for t in range(2):
        yq = lambda q: T.yt[:, 2 * q + t:2 * q + t + 1]
        ts(T.mk[:, 16 + t, 0:256], T.tc[:], yq(0), yq(3), ALU.is_gt, ALU.add, 128, ["tc", "yt"], ["sa%d" % t])
        ts(T.mk[:, 18 + t, 0:256], T.tc[:], yq(0), None, ALU.is_equal, None, 128, ["tc", "yt"], ["sb%d" % t])
        act(T.mk[:, 20 + t, 0:128], T.bo[:], 128, ["bo", "yt"], ["sc%d" % t], scale=yq(2))
        ts(T.mk[:, 22 + t, 0:128], T.rt[:], yq(1), yq(2), ALU.is_gt, ALU.mult, 64, ["rt", "yt"], ["sd%d" % t])
        mm(T.px[:, 0:256], T.mk[:, 20 + t, 0:128], T.mk[:, 16 + t, 0:256], False, False, 256, ["sa%d" % t, "sc%d" % t], "px")
        mm(T.px[:, 0:256], T.mk[:, 22 + t, 0:128], T.mk[:, 18 + t, 0:256], False, t == 1, 256, ["sb%d" % t, "sd%d" % t], "px")
    ts(T.off3[:], T.px[:, 0:256], col(G0), None, ALU.add, None, 256, ["g0"], ["off3"], ["px"])
    logs = ["ring"] + seven("log0_%d") + seven("log1_%d") + seven("log2_%d")
    parts, tag[0] = [], "scale"
    for c0, c1, q in CFG["scale"]:
        parts.append("part%d" % c0)
        if q == "s":
            act(T.win[:, c0:c1], T.raw[:, c0:c1], c1 - c0, ["ring"], parts[-1:], scale=1.0 / 256)
        else:
            ts(T.win[:, c0:c1], T.raw[:, c0:c1], 1.0 / 256, None, ALU.mult, None, (c1 - c0) / 2, ["ring"], parts[-1:])
    for e in range(3):
        packets(e, logs[:1 + 7 * e] + (parts if e else []))
    tag[0] = "out"
    for i, (c0, c1, q) in enumerate(CFG["ych"]):
        gather(q, T.yb[:, c0:c1], T.win[:], T.off3[:, c0 // 16:c1 // 16], c1 - c0, logs + parts + ["off3"], ["yb%d" % i],
               256.0 if scaled else None)
        dma("y", T.y[:, c0:c1], T.yb[:, c0:c1], "sty", ["yb%d" % i], ["st%d" % i], 1800.0 + 0.8 * (c1 - c0))
    tail = [(s, got[s]) for s in got]
    tail += [("ldh", 32), ("ldc", 16), ("ldd", 16), ("ldr", 16), ("ls", sent[0]), ("sty", 16 * (len(CFG["ych"]) + 1))]
    return ops, tail


def rank_program(g, core, T, topo):
    me = T.rank_of(core)
    if me is None:
        return
    ops, tail = build(T, topo, me)
    if "order" not in CFG:
        CFG["order"] = plan(ops)
    emit(g, T, ops, CFG["order"], tail)
